import numpy as np
import ml_dtypes


def mxq(x, axis, fmt="e4m3"):
    dtype, down = {"e4m3": (ml_dtypes.float8_e4m3fn, 7), "e5m2": (ml_dtypes.float8_e5m2, 14)}[fmt]
    v = np.moveaxis(np.asarray(x, np.float32).astype(ml_dtypes.bfloat16).astype(np.float64), axis, -1)
    blocks = v.reshape(v.shape[:-1] + (-1, 32))
    amax = np.abs(blocks).max(-1, keepdims=True)
    byte = np.maximum(np.where(amax > 0, np.frexp(amax)[1] - 1 + 127, 0) - down, 1)
    scale = np.exp2(byte - 127.0)
    codes = (blocks / scale).astype(np.float32).astype(dtype).astype(np.float64)
    return np.moveaxis((codes * scale).reshape(v.shape), -1, axis)


WIDE = False


def mx_kscale(k):
    if not WIDE:
        return np.ones(k)
    levels = np.array([10, -10, 5, -5, 0])
    if k % 512:
        return np.exp2(np.random.permutation(np.resize(levels, k // 32))).repeat(32)
    a = np.empty((k // 512, 16))
    for p in range(k // 512):
        a[p, :8] = np.random.permutation(np.resize(levels, 8))
        for g in range(8):
            far = levels[np.abs(levels - a[p, g]) >= 10]
            a[p, g + 8] = far[np.random.randint(len(far))]
    return np.exp2(a.ravel()).repeat(32)


def f64(x):
    return np.asarray(x).astype(np.float64)


def striped(idx):
    return np.tile(idx.reshape(-1, 16).T, (8, 1)).astype(np.uint16)


def unstriped(offs):
    return offs[:16].T.reshape(-1).astype(np.int64)


def pack_weight(w):
    k, n = w.shape
    w = f64(np.asarray(w, np.float32).astype(ml_dtypes.bfloat16)).reshape(k // 32, 32, n)
    amax = np.abs(w).max(1)
    byte = np.clip(np.where(amax > 0, np.frexp(amax)[1] - 1 + 127 - 7, 1), 1, 254)
    scaled = (w * np.exp2(127.0 - byte)[:, None, :]).reshape(k, n).astype(np.float32)
    words = np.ascontiguousarray(scaled.reshape(k // 512, 128, 4, n).transpose(0, 1, 3, 2)).astype(ml_dtypes.float8_e4m3fn).view(np.uint8)
    return words, np.ascontiguousarray(byte.astype(np.uint8).reshape(k // 512, 16, n))


def unpack_weight(words, scales):
    g, p, n, _ = words.shape
    vals = np.ascontiguousarray(words).view(ml_dtypes.float8_e4m3fn).astype(np.float64) * np.repeat(np.exp2(scales.astype(np.float64) - 127.0), 8, axis=1)[..., None]
    return vals.transpose(0, 1, 3, 2).reshape(g * 512, n)


def sigmoid(v):
    return 1.0 / (1.0 + np.exp(-np.maximum(v, -700.0)))


K, T, S, V = 1024, 2048, 512, 512


def setup_inputs():
    n = np.random.standard_normal
    s = mx_kscale(K)[:, None]
    packed_xT = pack_weight(n((K, T)) * s)
    return {
        "x_words": packed_xT[0],
        "x_scales": packed_xT[1],
        "hT": (n((K, V)) / np.sqrt(K) / s).astype(np.float32),
        "offs": striped(np.random.permutation(T)[:S]),
    }


def reference(x_words, x_scales, hT, offs):
    hTq = mxq(f64(hT), 0, "e4m3")
    xq = unpack_weight(x_words, x_scales)[:, unstriped(offs)]
    y = hTq.T @ xq
    a = sigmoid(y - 1.0)
    c0 = np.log(-1.0 * a + 1.001)
    c1 = c0 + np.pad(c0, ((0, 0), (1, 0)))[:, :S]
    c2 = c1 + np.pad(c1, ((0, 0), (2, 0)))[:, :S]
    c3 = c2 + np.pad(c2, ((0, 0), (4, 0)))[:, :S]
    return a * (np.exp(np.pad(c3, ((0, 0), (1, 0)))[:, :S]))

@@ -1,0 +1,161 @@
+from contextlib import ExitStack
+
+import concourse.mybir as mybir
+
+K, T, S, V = 1024, 2048, 512, 512
+FLOPS = 2 * K * S * V
+
+F32 = mybir.dt.float32
+BF16 = mybir.dt.bfloat16
+I32 = mybir.dt.int32
+U32 = mybir.dt.uint32
+U16 = mybir.dt.uint16
+U8 = mybir.dt.uint8
+FP8X4 = mybir.dt.float8_e4m3fn_x4
+ACT = mybir.ActivationFunctionType
+ALU = mybir.AluOpType
+
+P = 128
+PACK = 4
+PASSES = K // (P * PACK)
+BLOCKS = V // P
+HALF = S // 2
+WINDOW = 8
+KEEP = 1.001
+
+
+def tile_picked_ystick_eight_p_kernel(tc, x_words, x_scales, hT, offs, out):
+    nc = tc.nc
+    with ExitStack() as ctx:
+        pool = ctx.enter_context(tc.tile_pool(name="held", bufs=1))
+        psum = ctx.enter_context(tc.psum_pool(name="psum", bufs=1))
+
+        offsets = pool.tile([P, S // 16], U16, name="offsets")
+        scale_table = pool.tile([P, T], U8, name="scale_table", align_bytes=64)
+        word_table = [pool.tile([P, T], U32, name=f"word_table{g}", align_bytes=64) for g in range(PASSES)]
+        key_words = [pool.tile([P, S], U32, name=f"key_words{g}", align_bytes=64) for g in range(PASSES)]
+        key_scales = pool.tile([P, S], U8, name="key_scales", align_bytes=64)
+        h_raw = [[pool.tile([P, PACK, P], F32, name=f"h_raw{b}_{g}") for g in range(PASSES)] for b in range(BLOCKS)]
+        h_bf = [pool.tile([P, PASSES * P * PACK], BF16, name=f"h_bf{b}", align_bytes=64) for b in range(BLOCKS)]
+        h_words = [pool.tile([P, PASSES * P], U32, name=f"h_words{b}", align_bytes=64) for b in range(BLOCKS)]
+        h_scales = [pool.tile([P, PASSES * P], U8, name=f"h_scales{b}", align_bytes=64) for b in range(BLOCKS)]
+        share = [pool.tile([P, S], F32, name=f"share{b}") for b in range(BLOCKS)]
+        left = pool.tile([P, BLOCKS, WINDOW + S], F32, name="left")
+        left2 = [pool.tile([P, S + 6], F32, name=f"left2_{b}") for b in range(BLOCKS)]
+        left4 = [pool.tile([P, S + 4], F32, name=f"left4_{b}") for b in range(BLOCKS)]
+        left8 = [pool.tile([P, S], F32, name=f"left8_{b}") for b in range(BLOCKS)]
+        result = [pool.tile([P, S], F32, name=f"result{b}") for b in range(BLOCKS)]
+        minus_one = pool.tile([P, 1], F32, name="minus_one")
+        large = pool.tile([P, BLOCKS, WINDOW], F32, name="large")
+        scores = [[psum.tile([P, HALF], F32, name=f"scores{b}_{h}") for h in range(2)] for b in range(BLOCKS)]
+
+        nc.vector.memset(scale_table[:].bitcast(I32), 0)
+        nc.gpsimd.memset(large[:], 64.0)
+        nc.gpsimd.memset(minus_one[:], -1.0)
+        nc.scalar.activation(left[:, :, 0:WINDOW], large[:], ACT.Sigmoid)
+
+        def load_words(g):
+            nc.sync.dma_start(word_table[g][:].bitcast(I32), x_words[g].rearrange("p n t -> p (n t)").bitcast(I32))
+
+        def load_queries(b, g):
+            rows = hT[g * P * PACK : (g + 1) * P * PACK, b * P : (b + 1) * P]
+            nc.sync.dma_start(h_raw[b][g][:], rows.rearrange("(p j) v -> p j v", j=PACK))
+
+        def gather_words(g, h):
+            nc.vector.tensor_copy(
+                key_words[g][:, h * HALF : (h + 1) * HALF],
+                word_table[g][:].indirect(offsets[:, h * HALF // 16 : (h + 1) * HALF // 16]),
+            )
+
+        def round_queries(b, g, on_vector):
+            dst = h_bf[b][:, g * P * PACK : (g + 1) * P * PACK].rearrange("p (c i j) -> p c j i", i=4, j=PACK)
+            src = h_raw[b][g][:].rearrange("p j (c i) -> p c j i", i=4)
+            if on_vector:
+                nc.vector.tensor_copy(dst, src)
+            else:
+                nc.scalar.copy(dst, src)
+
+        def quantize_queries(b):
+            nc.vector.quantize_mx(out=h_words[b][:].bitcast(FP8X4), scales=h_scales[b][:], in_=h_bf[b][:])
+
+        def multiply(b, g, h):
+            keys = slice(h * HALF, (h + 1) * HALF)
+            nc.tensor.matmul_mx(
+                out=scores[b][h][:],
+                lhsT=h_words[b][:, g * P : (g + 1) * P].bitcast(FP8X4),
+                lhsT_scale=h_scales[b][:, g * P : (g + 1) * P],
+                rhs=key_words[g][:, keys].bitcast(FP8X4),
+                rhs_scale=key_scales[4 * g : P, keys],
+                start=(g == 0),
+                stop=(g == PASSES - 1),
+            )
+
+        def shares(b, h, on_vector):
+            keys = slice(h * HALF, (h + 1) * HALF)
+            nc.scalar.activation(share[b][:, keys], scores[b][h][:], ACT.Sigmoid, bias=minus_one[:])
+            dst = left[:, b, WINDOW + h * HALF : WINDOW + (h + 1) * HALF]
+            if on_vector:
+                nc.vector.tensor_scalar(dst, share[b][:, keys], -1.0, KEEP, ALU.mult, ALU.add)
+            else:
+                nc.scalar.activation(dst, share[b][:, keys], ACT.Copy, bias=KEEP, scale=-1.0)
+
+        def double(b, level, parts):
+            src = (left[:, b, :], left2[b][:], left4[b][:])[level]
+            dst = (left2[b][:], left4[b][:], left8[b][:])[level]
+            shift = 2**level
+            width = dst.shape[1]
+            cuts = (0, width) if parts == 1 else (0, width - HALF, width)
+            for lo, hi in zip(cuts, cuts[1:]):
+                nc.vector.tensor_tensor(dst[:, lo:hi], src[:, lo:hi], src[:, lo + shift : hi + shift], ALU.mult)
+
+        def finish(b, parts):
+            for h in range(parts):
+                keys = slice(h * S // parts, (h + 1) * S // parts)
+                nc.vector.tensor_tensor(result[b][:, keys], share[b][:, keys], left8[b][:, keys], ALU.mult)
+                nc.sync.dma_start(out[b * P : (b + 1) * P, keys], result[b][:, keys])
+
+        nc.sync.dma_start(offsets[:], offs)
+        load_words(0)
+        for q in range(4):
+            nc.scalar.dma_start(scale_table[32 * q : 32 * q + 8, :].bitcast(I32), x_scales[:, 4 * q : 4 * q + 4, :].bitcast(I32))
+        for g in range(PASSES):
+            load_queries(0, g)
+        load_words(1)
+        for b in range(1, BLOCKS):
+            for g in range(PASSES):
+                load_queries(b, g)
+
+        nc.vector.tensor_copy(key_scales[:], scale_table[:].indirect(offsets[:]))
+        for h in range(2):
+            gather_words(0, h)
+        round_queries(0, 0, False)
+        round_queries(0, 1, True)
+        quantize_queries(0)
+        for h in range(2):
+            multiply(0, 0, h)
+        for h in range(2):
+            gather_words(1, h)
+            multiply(0, 1, h)
+            shares(0, h, False)
+        def prepare(b):
+            for g in range(PASSES):
+                round_queries(b, g, b == 1 and g == 0)
+            quantize_queries(b)
+            for h in range(2):
+                for g in range(PASSES):
+                    multiply(b, g, h)
+
+        prepare(1)
+        double(0, 0, 2)
+        double(0, 1, 2)
+        for b in range(BLOCKS - 1):
+            for h in range(2):
+                shares(b + 1, h, False)
+            if b + 2 < BLOCKS:
+                prepare(b + 2)
+            double(b, 2, 1)
+            double(b + 1, 0, 1)
+            finish(b, 1)
+            double(b + 1, 1, 1)
+        double(BLOCKS - 1, 2, 2)
+        finish(BLOCKS - 1, 2)

@@ -109,13 +109,15 @@ def tile_picked_ystick_eight_p_kernel(tc, x_words, x_scales, hT, offs, out):
                 nc.vector.tensor_tensor(dst[:, lo:hi], src[:, lo:hi], src[:, lo + shift : hi + shift], ALU.mult)
 
         def finish(b, parts):
+            for h in range(2):
+                keys = slice(h * HALF, (h + 1) * HALF)
+                nc.vector.tensor_tensor(result[b][:, keys], share[b][:, keys], left8[b][:, keys], ALU.mult)
             for h in range(parts):
                 keys = slice(h * S // parts, (h + 1) * S // parts)
-                nc.vector.tensor_tensor(result[b][:, keys], share[b][:, keys], left8[b][:, keys], ALU.mult)
                 nc.sync.dma_start(out[b * P : (b + 1) * P, keys], result[b][:, keys])
 
-        nc.sync.dma_start(offsets[:], offs)
         load_words(0)
+        nc.sync.dma_start(offsets[:], offs)
         for q in range(4):
             nc.scalar.dma_start(scale_table[32 * q : 32 * q + 8, :].bitcast(I32), x_scales[:, 4 * q : 4 * q + 4, :].bitcast(I32))
         for g in range(PASSES):
@@ -136,7 +138,7 @@ def tile_picked_ystick_eight_p_kernel(tc, x_words, x_scales, hT, offs, out):
         for h in range(2):
             gather_words(1, h)
             multiply(0, 1, h)
-            shares(0, h, False)
+            shares(0, h, True)
         def prepare(b):
             for g in range(PASSES):
                 round_queries(b, g, b == 1 and g == 0)
@@ -145,17 +147,12 @@ def tile_picked_ystick_eight_p_kernel(tc, x_words, x_scales, hT, offs, out):
                 for g in range(PASSES):
                     multiply(b, g, h)
 
-        prepare(1)
-        double(0, 0, 2)
-        double(0, 1, 2)
-        for b in range(BLOCKS - 1):
-            for h in range(2):
-                shares(b + 1, h, False)
-            if b + 2 < BLOCKS:
-                prepare(b + 2)
-            double(b, 2, 1)
-            double(b + 1, 0, 1)
-            finish(b, 1)
-            double(b + 1, 1, 1)
-        double(BLOCKS - 1, 2, 2)
-        finish(BLOCKS - 1, 2)
+        for b in range(BLOCKS):
+            if b + 1 < BLOCKS:
+                prepare(b + 1)
+            for level in range(3):
+                double(b, level, 2)
+            finish(b, 2 if b + 1 == BLOCKS else 1)
+            if b + 1 < BLOCKS:
+                for h in range(2):
+                    shares(b + 1, h, False)

@@ -28,26 +28,30 @@ def tile_picked_ystick_eight_p_kernel(tc, x_words, x_scales, hT, offs, out):
     nc = tc.nc
     with ExitStack() as ctx:
         pool = ctx.enter_context(tc.tile_pool(name="held", bufs=1))
+        reused = ctx.enter_context(tc.tile_pool(name="reused", bufs=1))
         psum = ctx.enter_context(tc.psum_pool(name="psum", bufs=1))
+
+        KIB = 1024
+        at_words1, at_codes0, at_scales0, at_round0, at_left8 = 0, 8 * KIB, 9 * KIB, 10 * KIB, 12 * KIB
+
+        def placed(shape, dtype, name, offset):
+            return reused.tile(shape, dtype, name=name, offset=offset, align_bytes=64)
 
         offsets = pool.tile([P, S // 16], U16, name="offsets")
         scale_table = pool.tile([P, T], U8, name="scale_table", align_bytes=64)
-        word_table = [pool.tile([P, T], U32, name=f"word_table{g}", align_bytes=64) for g in range(PASSES)]
-        key_words = [pool.tile([P, S], U32, name=f"key_words{g}", align_bytes=64) for g in range(PASSES)]
+        word_table = [pool.tile([P, T], U32, name="word_table0", align_bytes=64), placed([P, T], U32, "word_table1", at_words1)]
         key_scales = pool.tile([P, S], U8, name="key_scales", align_bytes=64)
-        h_raw = [[pool.tile([P, PACK, P], F32, name=f"h_raw{b}_{g}") for g in range(PASSES)] for b in range(BLOCKS)]
-        h_bf = [pool.tile([P, PASSES * P * PACK], BF16, name=f"h_bf{b}", align_bytes=64) for b in range(BLOCKS)]
-        h_words = [pool.tile([P, PASSES * P], U32, name=f"h_words{b}", align_bytes=64) for b in range(BLOCKS)]
-        h_scales = [pool.tile([P, PASSES * P], U8, name=f"h_scales{b}", align_bytes=64) for b in range(BLOCKS)]
+        h_raw = {(g, b): pool.tile([P, PACK, P], F32, name=f"h_raw{g}_{b}") for b in range(BLOCKS) for g in range(PASSES)}
         share = [pool.tile([P, S], F32, name=f"share{b}") for b in range(BLOCKS)]
         left = pool.tile([P, BLOCKS, WINDOW + S], F32, name="left")
         left2 = [pool.tile([P, S + 6], F32, name=f"left2_{b}") for b in range(BLOCKS)]
         left4 = [pool.tile([P, S + 4], F32, name=f"left4_{b}") for b in range(BLOCKS)]
-        left8 = [pool.tile([P, S], F32, name=f"left8_{b}") for b in range(BLOCKS)]
+        left8 = [placed([P, S], F32, f"left8_{b}", at_left8 + 2 * KIB * b) for b in range(BLOCKS)]
         result = [pool.tile([P, S], F32, name=f"result{b}") for b in range(BLOCKS)]
         minus_one = pool.tile([P, 1], F32, name="minus_one")
         large = pool.tile([P, BLOCKS, WINDOW], F32, name="large")
         scores = [[psum.tile([P, HALF], F32, name=f"scores{b}_{h}") for h in range(2)] for b in range(BLOCKS)]
+        key_words, h_bf, h_words, h_scales = {}, {}, {}, {}
 
         nc.vector.memset(scale_table[:].bitcast(I32), 0)
         nc.gpsimd.memset(large[:], 64.0)
@@ -57,102 +61,146 @@ def tile_picked_ystick_eight_p_kernel(tc, x_words, x_scales, hT, offs, out):
         def load_words(g):
             nc.sync.dma_start(word_table[g][:].bitcast(I32), x_words[g].rearrange("p n t -> p (n t)").bitcast(I32))
 
-        def load_queries(b, g):
+        def load_queries(g, b):
             rows = hT[g * P * PACK : (g + 1) * P * PACK, b * P : (b + 1) * P]
-            nc.sync.dma_start(h_raw[b][g][:], rows.rearrange("(p j) v -> p j v", j=PACK))
+            nc.sync.dma_start(h_raw[g, b][:], rows.rearrange("(p j) v -> p j v", j=PACK))
 
-        def gather_words(g, h):
-            nc.vector.tensor_copy(
-                key_words[g][:, h * HALF : (h + 1) * HALF],
-                word_table[g][:].indirect(offsets[:, h * HALF // 16 : (h + 1) * HALF // 16]),
-            )
+        def gather_words(target, g, lo, hi):
+            nc.vector.tensor_copy(target, word_table[g][:].indirect(offsets[:, lo // 16 : hi // 16]))
 
-        def round_queries(b, g, on_vector):
-            dst = h_bf[b][:, g * P * PACK : (g + 1) * P * PACK].rearrange("p (c i j) -> p c j i", i=4, j=PACK)
-            src = h_raw[b][g][:].rearrange("p j (c i) -> p c j i", i=4)
+        def round_queries(g, b, on_vector):
+            dst = h_bf[g, b].rearrange("p (c i j) -> p c j i", i=4, j=PACK)
+            src = h_raw[g, b][:].rearrange("p j (c i) -> p c j i", i=4)
             if on_vector:
                 nc.vector.tensor_copy(dst, src)
             else:
                 nc.scalar.copy(dst, src)
 
-        def quantize_queries(b):
-            nc.vector.quantize_mx(out=h_words[b][:].bitcast(FP8X4), scales=h_scales[b][:], in_=h_bf[b][:])
-
         def multiply(b, g, h):
             keys = slice(h * HALF, (h + 1) * HALF)
             nc.tensor.matmul_mx(
                 out=scores[b][h][:],
-                lhsT=h_words[b][:, g * P : (g + 1) * P].bitcast(FP8X4),
-                lhsT_scale=h_scales[b][:, g * P : (g + 1) * P],
-                rhs=key_words[g][:, keys].bitcast(FP8X4),
+                lhsT=h_words[g, b].bitcast(FP8X4),
+                lhsT_scale=h_scales[g, b],
+                rhs=key_words[g, h].bitcast(FP8X4),
                 rhs_scale=key_scales[4 * g : P, keys],
                 start=(g == 0),
                 stop=(g == PASSES - 1),
             )
 
-        def shares(b, h, on_vector):
+        def round_into(g, b, offset, on_vector):
+            h_bf[g, b] = placed([P, P * PACK], BF16, f"h_bf{g}_{b}", offset)[:]
+            round_queries(g, b, on_vector)
+
+        def quantize(g, b):
+            h_words[g, b] = pool.tile([P, P], U32, name=f"h_words{g}_{b}", align_bytes=64)[:]
+            h_scales[g, b] = pool.tile([P, P], U8, name=f"h_scales{g}_{b}", align_bytes=64)[:]
+            nc.vector.quantize_mx(out=h_words[g, b].bitcast(FP8X4), scales=h_scales[g, b], in_=h_bf[g, b])
+            for h in range(2):
+                multiply(b, g, h)
+
+        def sigmoid(b, h):
+            nc.scalar.activation(share[b][:, h * HALF : (h + 1) * HALF], scores[b][h][:], ACT.Sigmoid, bias=minus_one[:])
+
+        def factor(b, h, on_vector):
             keys = slice(h * HALF, (h + 1) * HALF)
-            nc.scalar.activation(share[b][:, keys], scores[b][h][:], ACT.Sigmoid, bias=minus_one[:])
-            dst = left[:, b, WINDOW + h * HALF : WINDOW + (h + 1) * HALF]
+            dst = left[:, b, WINDOW + keys.start : WINDOW + keys.stop]
             if on_vector:
                 nc.vector.tensor_scalar(dst, share[b][:, keys], -1.0, KEEP, ALU.mult, ALU.add)
             else:
                 nc.scalar.activation(dst, share[b][:, keys], ACT.Copy, bias=KEEP, scale=-1.0)
 
-        def double(b, level, parts):
-            src = (left[:, b, :], left2[b][:], left4[b][:])[level]
-            dst = (left2[b][:], left4[b][:], left8[b][:])[level]
-            shift = 2**level
-            width = dst.shape[1]
-            cuts = (0, width) if parts == 1 else (0, width - HALF, width)
-            for lo, hi in zip(cuts, cuts[1:]):
-                nc.vector.tensor_tensor(dst[:, lo:hi], src[:, lo:hi], src[:, lo + shift : hi + shift], ALU.mult)
-
-        def finish(b, parts):
+        def shares(b):
             for h in range(2):
-                keys = slice(h * HALF, (h + 1) * HALF)
-                nc.vector.tensor_tensor(result[b][:, keys], share[b][:, keys], left8[b][:, keys], ALU.mult)
-            for h in range(parts):
-                keys = slice(h * S // parts, (h + 1) * S // parts)
-                nc.sync.dma_start(out[b * P : (b + 1) * P, keys], result[b][:, keys])
+                sigmoid(b, h)
+                factor(b, h, False)
+
+        def product(b, level, h):
+            src = (left[:, b, :], left2[b][:], left4[b][:], left8[b][:])[level]
+            dst = (left2[b][:], left4[b][:], left8[b][:], result[b][:])[level]
+            width = dst.shape[1]
+            lo, hi = ((0, width - HALF), (width - HALF, width))[h]
+            other = share[b][:, lo:hi] if level == 3 else src[:, lo + 2**level : hi + 2**level]
+            nc.vector.tensor_tensor(dst[:, lo:hi], src[:, lo:hi], other, ALU.mult)
+
+        def store(b, lo, hi):
+            nc.sync.dma_start(out[b * P : (b + 1) * P, lo:hi], result[b][:, lo:hi])
+
+        def products(b, levels):
+            for level in levels:
+                for h in range(2):
+                    product(b, level, h)
 
         load_words(0)
         nc.sync.dma_start(offsets[:], offs)
+        load_queries(0, 0)
         for q in range(4):
-            nc.scalar.dma_start(scale_table[32 * q : 32 * q + 8, :].bitcast(I32), x_scales[:, 4 * q : 4 * q + 4, :].bitcast(I32))
-        for g in range(PASSES):
-            load_queries(0, g)
+            nc.sync.dma_start(scale_table[32 * q : 32 * q + 8, :].bitcast(I32), x_scales[:, 4 * q : 4 * q + 4, :].bitcast(I32))
+        load_queries(1, 0)
         load_words(1)
         for b in range(1, BLOCKS):
             for g in range(PASSES):
-                load_queries(b, g)
+                load_queries(g, b)
 
-        nc.vector.tensor_copy(key_scales[:], scale_table[:].indirect(offsets[:]))
+        first_keys = pool.tile([P, S], U32, name="first_keys", align_bytes=64)
+        gather_words(first_keys[:], 0, 0, S)
         for h in range(2):
-            gather_words(0, h)
-        round_queries(0, 0, False)
-        round_queries(0, 1, True)
-        quantize_queries(0)
+            key_words[0, h] = first_keys[:, h * HALF : (h + 1) * HALF]
+        nc.vector.tensor_copy(key_scales[:], scale_table[:].indirect(offsets[:]))
+
+        first_bf = placed([P, PASSES * P * PACK], BF16, "first_bf", at_round0)
+        first_words = placed([P, PASSES * P], U32, "first_words", at_codes0)
+        first_scales = placed([P, PASSES * P], U8, "first_scales", at_scales0)
+        for g in range(PASSES):
+            h_bf[g, 0] = first_bf[:, g * P * PACK : (g + 1) * P * PACK]
+            h_words[g, 0] = first_words[:, g * P : (g + 1) * P]
+            h_scales[g, 0] = first_scales[:, g * P : (g + 1) * P]
+            round_queries(g, 0, False)
+        nc.vector.quantize_mx(out=first_words[:].bitcast(FP8X4), scales=first_scales[:], in_=first_bf[:])
         for h in range(2):
             multiply(0, 0, h)
-        for h in range(2):
-            gather_words(1, h)
-            multiply(0, 1, h)
-            shares(0, h, True)
-        def prepare(b):
-            for g in range(PASSES):
-                round_queries(b, g, b == 1 and g == 0)
-            quantize_queries(b)
-            for h in range(2):
-                for g in range(PASSES):
-                    multiply(b, g, h)
 
-        for b in range(BLOCKS):
-            if b + 1 < BLOCKS:
-                prepare(b + 1)
-            for level in range(3):
-                double(b, level, 2)
-            finish(b, 2 if b + 1 == BLOCKS else 1)
-            if b + 1 < BLOCKS:
-                for h in range(2):
-                    shares(b + 1, h, False)
+        for h in range(2):
+            key_words[1, h] = placed([P, HALF], U32, f"second_keys{h}", at_round0 + h * KIB)[:]
+            gather_words(key_words[1, h], 1, h * HALF, (h + 1) * HALF)
+            multiply(0, 1, h)
+            sigmoid(0, h)
+        round_into(0, 1, at_words1, True)
+        round_into(1, 1, at_codes0, False)
+        round_into(0, 2, at_scales0, False)
+        factor(0, 0, True)
+        product(0, 0, 0)
+        product(0, 1, 0)
+        quantize(0, 1)
+        factor(0, 1, True)
+        quantize(1, 1)
+        shares(1)
+        product(0, 0, 1)
+        product(0, 2, 0)
+        product(0, 1, 1)
+        product(0, 3, 0)
+        product(0, 2, 1)
+        quantize(0, 2)
+        product(0, 3, 1)
+        store(0, 0, S)
+
+        round_into(1, 2, at_left8, False)
+        round_into(0, 3, at_left8 + KIB, False)
+        products(1, (0,))
+        quantize(1, 2)
+        shares(2)
+        products(1, (1, 2))
+        quantize(0, 3)
+        products(1, (3,))
+        store(1, 0, S)
+
+        round_into(1, 3, at_left8 + 2 * KIB, False)
+        products(2, (0,))
+        quantize(1, 3)
+        shares(3)
+        products(2, (1, 2, 3))
+        store(2, 0, S)
+
+        products(3, (0, 1, 2, 3))
+        store(3, 0, HALF)
+        store(3, HALF, S)

@@ -32,13 +32,14 @@ def tile_picked_ystick_eight_p_kernel(tc, x_words, x_scales, hT, offs, out):
         psum = ctx.enter_context(tc.psum_pool(name="psum", bufs=1))
 
         KIB = 1024
-        at_words1, at_codes0, at_scales0, at_round0, at_left8 = 0, 8 * KIB, 9 * KIB, 10 * KIB, 12 * KIB
+        at_words1, at_codes0, at_scales0, at_round0, at_planes0, at_left8 = 0, 8 * KIB, 9 * KIB, 11 * KIB, 13 * KIB, 20 * KIB
+        at_codes1, at_codes2 = 15 * KIB, 17 * KIB
 
         def placed(shape, dtype, name, offset):
             return reused.tile(shape, dtype, name=name, offset=offset, align_bytes=64)
 
         offsets = pool.tile([P, S // 16], U16, name="offsets")
-        scale_table = pool.tile([P, T], U8, name="scale_table", align_bytes=64)
+        scale_table = placed([P, T], U8, "scale_table", at_scales0)
         word_table = [pool.tile([P, T], U32, name="word_table0", align_bytes=64), placed([P, T], U32, "word_table1", at_words1)]
         key_scales = pool.tile([P, S], U8, name="key_scales", align_bytes=64)
         h_raw = {(g, b): pool.tile([P, PACK, P], F32, name=f"h_raw{g}_{b}") for b in range(BLOCKS) for g in range(PASSES)}
@@ -58,8 +59,9 @@ def tile_picked_ystick_eight_p_kernel(tc, x_words, x_scales, hT, offs, out):
         nc.gpsimd.memset(minus_one[:], -1.0)
         nc.scalar.activation(left[:, :, 0:WINDOW], large[:], ACT.Sigmoid)
 
-        def load_words(g):
-            nc.sync.dma_start(word_table[g][:].bitcast(I32), x_words[g].rearrange("p n t -> p (n t)").bitcast(I32))
+        def load_words(g, lo, hi):
+            words = x_words[g].rearrange("p n t -> p (n t)").bitcast(I32)
+            nc.sync.dma_start(word_table[g][:, lo:hi].bitcast(I32), words[:, lo:hi])
 
         def load_queries(g, b):
             rows = hT[g * P * PACK : (g + 1) * P * PACK, b * P : (b + 1) * P]
@@ -87,17 +89,6 @@ def tile_picked_ystick_eight_p_kernel(tc, x_words, x_scales, hT, offs, out):
                 start=(g == 0),
                 stop=(g == PASSES - 1),
             )
-
-        def round_into(g, b, offset, on_vector):
-            h_bf[g, b] = placed([P, P * PACK], BF16, f"h_bf{g}_{b}", offset)[:]
-            round_queries(g, b, on_vector)
-
-        def quantize(g, b):
-            h_words[g, b] = pool.tile([P, P], U32, name=f"h_words{g}_{b}", align_bytes=64)[:]
-            h_scales[g, b] = pool.tile([P, P], U8, name=f"h_scales{g}_{b}", align_bytes=64)[:]
-            nc.vector.quantize_mx(out=h_words[g, b].bitcast(FP8X4), scales=h_scales[g, b], in_=h_bf[g, b])
-            for h in range(2):
-                multiply(b, g, h)
 
         def sigmoid(b, h):
             nc.scalar.activation(share[b][:, h * HALF : (h + 1) * HALF], scores[b][h][:], ACT.Sigmoid, bias=minus_one[:])
@@ -131,13 +122,14 @@ def tile_picked_ystick_eight_p_kernel(tc, x_words, x_scales, hT, offs, out):
                 for h in range(2):
                     product(b, level, h)
 
-        load_words(0)
-        nc.sync.dma_start(offsets[:], offs)
+        load_words(0, 0, T // 2)
         load_queries(0, 0)
+        load_words(0, T // 2, T)
+        nc.sync.dma_start(offsets[:], offs)
         for q in range(4):
             nc.sync.dma_start(scale_table[32 * q : 32 * q + 8, :].bitcast(I32), x_scales[:, 4 * q : 4 * q + 4, :].bitcast(I32))
         load_queries(1, 0)
-        load_words(1)
+        load_words(1, 0, T)
         for b in range(1, BLOCKS):
             for g in range(PASSES):
                 load_queries(g, b)
@@ -150,7 +142,7 @@ def tile_picked_ystick_eight_p_kernel(tc, x_words, x_scales, hT, offs, out):
 
         first_bf = placed([P, PASSES * P * PACK], BF16, "first_bf", at_round0)
         first_words = placed([P, PASSES * P], U32, "first_words", at_codes0)
-        first_scales = placed([P, PASSES * P], U8, "first_scales", at_scales0)
+        first_scales = placed([P, PASSES * P], U8, "first_scales", at_planes0)
         for g in range(PASSES):
             h_bf[g, 0] = first_bf[:, g * P * PACK : (g + 1) * P * PACK]
             h_words[g, 0] = first_words[:, g * P : (g + 1) * P]
@@ -161,46 +153,77 @@ def tile_picked_ystick_eight_p_kernel(tc, x_words, x_scales, hT, offs, out):
             multiply(0, 0, h)
 
         for h in range(2):
-            key_words[1, h] = placed([P, HALF], U32, f"second_keys{h}", at_round0 + h * KIB)[:]
+            key_words[1, h] = placed([P, HALF], U32, f"second_keys{h}", at_round0 - KIB // 2 + h * KIB)[:]
             gather_words(key_words[1, h], 1, h * HALF, (h + 1) * HALF)
             multiply(0, 1, h)
             sigmoid(0, h)
-        round_into(0, 1, at_words1, True)
-        round_into(1, 1, at_codes0, False)
-        round_into(0, 2, at_scales0, False)
+        def quantize_block(b, offset):
+            words = placed([P, PASSES * P], U32, f"h_words{b}", offset)
+            planes = pool.tile([P, PASSES * P], U8, name=f"h_scales{b}", align_bytes=64)
+            nc.vector.quantize_mx(out=words[:].bitcast(FP8X4), scales=planes[:], in_=rounded[b][:])
+            for g in range(PASSES):
+                h_words[g, b] = words[:, g * P : (g + 1) * P]
+                h_scales[g, b] = planes[:, g * P : (g + 1) * P]
+            for h in range(2):
+                for g in range(PASSES):
+                    multiply(b, g, h)
+
+        def round_block(b, offset, on_vector):
+            rounded[b] = placed([P, PASSES * P * PACK], BF16, f"rounded{b}", offset)
+            for g in range(PASSES):
+                h_bf[g, b] = rounded[b][:, g * P * PACK : (g + 1) * P * PACK]
+                round_queries(g, b, on_vector[g])
+
+        def whole(b, level):
+            src = (left[:, b, :], left2[b][:], left4[b][:], left8[b][:])[level]
+            dst = (left2[b][:], left4[b][:], left8[b][:], result[b][:])[level]
+            width = dst.shape[1]
+            other = share[b][:] if level == 3 else src[:, 2**level : width + 2**level]
+            nc.vector.tensor_tensor(dst, src[:, 0:width], other, ALU.mult)
+
+        def quantize_pass(g, b, offset):
+            h_words[g, b] = placed([P, P], U32, f"h_words{g}_{b}", offset)[:]
+            h_scales[g, b] = pool.tile([P, P], U8, name=f"h_scales{g}_{b}", align_bytes=64)[:]
+            nc.vector.quantize_mx(out=h_words[g, b].bitcast(FP8X4), scales=h_scales[g, b], in_=h_bf[g, b])
+            for h in range(2):
+                multiply(b, g, h)
+
+        rounded = {}
+        h_bf[0, 1] = placed([P, P * PACK], BF16, "rounded0_1", at_scales0)[:]
+        h_bf[1, 1] = placed([P, P * PACK], BF16, "rounded1_1", at_words1)[:]
+        round_queries(0, 1, False)
+        quantize_pass(0, 1, at_words1 + KIB)
+        round_queries(1, 1, True)
         factor(0, 0, True)
+        quantize_pass(1, 1, at_codes1)
         product(0, 0, 0)
         product(0, 1, 0)
-        quantize(0, 1)
-        factor(0, 1, True)
-        quantize(1, 1)
+        factor(0, 1, False)
+        round_block(2, at_planes0, (False, False))
         shares(1)
+        round_block(3, at_codes1, (False, False))
         product(0, 0, 1)
         product(0, 2, 0)
         product(0, 1, 1)
         product(0, 3, 0)
         product(0, 2, 1)
-        quantize(0, 2)
+        quantize_block(2, at_codes2)
         product(0, 3, 1)
         store(0, 0, S)
-
-        round_into(1, 2, at_left8, False)
-        round_into(0, 3, at_left8 + KIB, False)
-        products(1, (0,))
-        quantize(1, 2)
         shares(2)
-        products(1, (1, 2))
-        quantize(0, 3)
-        products(1, (3,))
+
+        products(1, (0, 1))
+        quantize_block(3, at_codes2 + KIB)
+        shares(3)
+        products(1, (2, 3))
         store(1, 0, S)
 
-        round_into(1, 3, at_left8 + 2 * KIB, False)
-        products(2, (0,))
-        quantize(1, 3)
-        shares(3)
-        products(2, (1, 2, 3))
+        products(2, (0, 1))
+        whole(3, 0)
+        whole(2, 2)
+        whole(3, 1)
+        whole(2, 3)
         store(2, 0, S)
-
-        products(3, (0, 1, 2, 3))
+        products(3, (2, 3))
         store(3, 0, HALF)
         store(3, HALF, S)

@@ -51,7 +51,8 @@ def tile_picked_ystick_eight_p_kernel(tc, x_words, x_scales, hT, offs, out):
         result = [pool.tile([P, S], F32, name=f"result{b}") for b in range(BLOCKS)]
         minus_one = pool.tile([P, 1], F32, name="minus_one")
         large = pool.tile([P, BLOCKS, WINDOW], F32, name="large")
-        scores = [[psum.tile([P, HALF], F32, name=f"scores{b}_{h}") for h in range(2)] for b in range(BLOCKS)]
+        banks = [[psum.tile([P, S], F32, name=f"scores{b}_{h}") for h in range(2)] for b in range(BLOCKS)]
+        scores = [[bank[:, 0:HALF] for bank in pair] for pair in banks]
         key_words, h_bf, h_words, h_scales = {}, {}, {}, {}
 
         nc.vector.memset(scale_table[:].bitcast(I32), 0)
@@ -81,7 +82,7 @@ def tile_picked_ystick_eight_p_kernel(tc, x_words, x_scales, hT, offs, out):
         def multiply(b, g, h):
             keys = slice(h * HALF, (h + 1) * HALF)
             nc.tensor.matmul_mx(
-                out=scores[b][h][:],
+                out=scores[b][h],
                 lhsT=h_words[g, b].bitcast(FP8X4),
                 lhsT_scale=h_scales[g, b],
                 rhs=key_words[g, h].bitcast(FP8X4),
@@ -91,7 +92,7 @@ def tile_picked_ystick_eight_p_kernel(tc, x_words, x_scales, hT, offs, out):
             )
 
         def sigmoid(b, h):
-            nc.scalar.activation(share[b][:, h * HALF : (h + 1) * HALF], scores[b][h][:], ACT.Sigmoid, bias=minus_one[:])
+            nc.scalar.activation(share[b][:, h * HALF : (h + 1) * HALF], scores[b][h], ACT.Sigmoid, bias=minus_one[:])
 
         def factor(b, h, on_vector):
             keys = slice(h * HALF, (h + 1) * HALF)
@@ -151,6 +152,15 @@ def tile_picked_ystick_eight_p_kernel(tc, x_words, x_scales, hT, offs, out):
         nc.vector.quantize_mx(out=first_words[:].bitcast(FP8X4), scales=first_scales[:], in_=first_bf[:])
         for h in range(2):
             multiply(0, 0, h)
+        nc.tensor.matmul_mx(
+            out=banks[3][1][:],
+            lhsT=h_words[0, 0].bitcast(FP8X4),
+            lhsT_scale=h_scales[0, 0],
+            rhs=first_keys[:].bitcast(FP8X4),
+            rhs_scale=key_scales[:],
+            start=True,
+            stop=True,
+        )
 
         for h in range(2):
             key_words[1, h] = placed([P, HALF], U32, f"second_keys{h}", at_round0 - KIB // 2 + h * KIB)[:]

@@ -20,7 +20,11 @@ PACK = 4
 PASSES = K // (P * PACK)
 BLOCKS = V // P
 HALF = S // 2
-WINDOW = 8
+QUARTER = S // 4
+LEAD = 4
+GROUP = 4
+GROUPS = S // GROUP
+ROW = LEAD + GROUPS
 KEEP = 1.001
 
 
@@ -32,8 +36,8 @@ def tile_picked_ystick_eight_p_kernel(tc, x_words, x_scales, hT, offs, out):
         psum = ctx.enter_context(tc.psum_pool(name="psum", bufs=1))
 
         KIB = 1024
-        at_words1, at_codes0, at_scales0, at_round0, at_planes0, at_left8 = 0, 8 * KIB, 9 * KIB, 11 * KIB, 13 * KIB, 20 * KIB
-        at_codes1, at_codes2 = 15 * KIB, 17 * KIB
+        at_words1, at_codes0, at_scales0, at_round0, at_planes0 = 0, 8 * KIB, 9 * KIB, 11 * KIB, 13 * KIB
+        at_codes1, at_codes2, at_raw = 15 * KIB, 17 * KIB, 20 * KIB
 
         def placed(shape, dtype, name, offset):
             return reused.tile(shape, dtype, name=name, offset=offset, align_bytes=64)
@@ -42,23 +46,33 @@ def tile_picked_ystick_eight_p_kernel(tc, x_words, x_scales, hT, offs, out):
         scale_table = placed([P, T], U8, "scale_table", at_scales0)
         word_table = [pool.tile([P, T], U32, name="word_table0", align_bytes=64), placed([P, T], U32, "word_table1", at_words1)]
         key_scales = pool.tile([P, S], U8, name="key_scales", align_bytes=64)
-        h_raw = {(g, b): pool.tile([P, PACK, P], F32, name=f"h_raw{g}_{b}") for b in range(BLOCKS) for g in range(PASSES)}
-        share = [pool.tile([P, S], F32, name=f"share{b}") for b in range(BLOCKS)]
-        left = pool.tile([P, BLOCKS, WINDOW + S], F32, name="left")
-        left2 = [pool.tile([P, S + 6], F32, name=f"left2_{b}") for b in range(BLOCKS)]
-        left4 = [pool.tile([P, S + 4], F32, name=f"left4_{b}") for b in range(BLOCKS)]
-        left8 = [placed([P, S], F32, f"left8_{b}", at_left8 + 2 * KIB * b) for b in range(BLOCKS)]
+        h_raw = {(g, b): placed([P, PACK, P], F32, f"h_raw{g}_{b}", at_raw + 2 * KIB * (PASSES * b + g)) for b in range(BLOCKS) for g in range(PASSES)}
+        later = range(1, BLOCKS)
+        first_share = pool.tile([P, LEAD + S], F32, name="first_share")
+        even = pool.tile([P, LEAD + HALF], F32, name="even")
+        left2 = pool.tile([P, 2, LEAD + HALF], F32, name="left2")
+        left4 = pool.tile([P, 2, LEAD + HALF], F32, name="left4")
+        left8 = pool.tile([P, 2, HALF], F32, name="left8")
+        share = {1: placed([P, GROUP, GROUPS], F32, "share1", at_raw + 2 * KIB * (PASSES * 2 + 1))}
+        share.update({b: pool.tile([P, GROUP, GROUPS], F32, name=f"share{b}") for b in range(2, BLOCKS)})
+        chains = pool.tile([P, BLOCKS - 1, 3 * GROUP + 1, ROW], F32, name="chains")
+        window = {b: pool.tile([P, GROUP, GROUPS], F32, name=f"window{b}") for b in later}
         result = [pool.tile([P, S], F32, name=f"result{b}") for b in range(BLOCKS)]
         minus_one = pool.tile([P, 1], F32, name="minus_one")
-        large = pool.tile([P, BLOCKS, WINDOW], F32, name="large")
-        banks = [[psum.tile([P, S], F32, name=f"scores{b}_{h}") for h in range(2)] for b in range(BLOCKS)]
-        scores = [[bank[:, 0:HALF] for bank in pair] for pair in banks]
+        large = pool.tile([P, 1], F32, name="large")
+        first_scores = [psum.tile([P, S], F32, name=f"first_scores{h}")[:, 0:HALF] for h in range(2)]
+        scores = {b: psum.tile([P, S], F32, name=f"scores{b}") for b in later}
+        spare = psum.tile([P, S], F32, name="spare")
         key_words, h_bf, h_words, h_scales = {}, {}, {}, {}
 
         nc.vector.memset(scale_table[:].bitcast(I32), 0)
         nc.gpsimd.memset(large[:], 64.0)
         nc.gpsimd.memset(minus_one[:], -1.0)
-        nc.scalar.activation(left[:, :, 0:WINDOW], large[:], ACT.Sigmoid)
+        nc.vector.memset(left2[:, :, 1:LEAD], -1.0)
+        nc.vector.memset(chains[:, :, 0:GROUP:2, LEAD - 2 : LEAD], 1.0)
+        nc.vector.memset(chains[:, :, 1:GROUP:2, LEAD - 2 : LEAD], -1.0)
+        nc.scalar.activation(even[:, LEAD - 1 : LEAD], large[:], ACT.Sigmoid)
+        nc.scalar.activation(first_share[:, LEAD - 1 : LEAD], even[:, LEAD - 1 : LEAD], ACT.Copy, scale=KEEP - 1.0)
 
         def load_words(g, lo, hi):
             words = x_words[g].rearrange("p n t -> p (n t)").bitcast(I32)
@@ -79,54 +93,103 @@ def tile_picked_ystick_eight_p_kernel(tc, x_words, x_scales, hT, offs, out):
             else:
                 nc.scalar.copy(dst, src)
 
-        def multiply(b, g, h):
-            keys = slice(h * HALF, (h + 1) * HALF)
+        def multiply(target, b, g, keys, lo, hi):
             nc.tensor.matmul_mx(
-                out=scores[b][h],
+                out=target,
                 lhsT=h_words[g, b].bitcast(FP8X4),
                 lhsT_scale=h_scales[g, b],
-                rhs=key_words[g, h].bitcast(FP8X4),
-                rhs_scale=key_scales[4 * g : P, keys],
+                rhs=keys.bitcast(FP8X4),
+                rhs_scale=key_scales[4 * g : P, lo:hi],
                 start=(g == 0),
                 stop=(g == PASSES - 1),
             )
 
-        def sigmoid(b, h):
-            nc.scalar.activation(share[b][:, h * HALF : (h + 1) * HALF], scores[b][h], ACT.Sigmoid, bias=minus_one[:])
+        def multiply_pass(b, g):
+            for h in range(2):
+                nc.tensor.matmul_mx(
+                    out=scores[b][:, h * HALF : (h + 1) * HALF],
+                    lhsT=h_words[g, b].bitcast(FP8X4),
+                    lhsT_scale=h_scales[g, b],
+                    rhs=key_words[g, h].bitcast(FP8X4),
+                    rhs_scale=key_scales[4 * g : P, h * HALF : (h + 1) * HALF],
+                    start=(g == 0 and h == 0),
+                    stop=(g == PASSES - 1 and h == 1),
+                )
 
-        def factor(b, h, on_vector):
-            keys = slice(h * HALF, (h + 1) * HALF)
-            dst = left[:, b, WINDOW + keys.start : WINDOW + keys.stop]
+        def factor(h, on_vector):
+            src = first_share[:, LEAD + h * HALF : LEAD + (h + 1) * HALF : 2]
+            dst = even[:, LEAD + h * QUARTER : LEAD + (h + 1) * QUARTER]
             if on_vector:
-                nc.vector.tensor_scalar(dst, share[b][:, keys], -1.0, KEEP, ALU.mult, ALU.add)
+                nc.vector.tensor_scalar(dst, src, -1.0, KEEP, ALU.mult, ALU.add)
             else:
-                nc.scalar.activation(dst, share[b][:, keys], ACT.Copy, bias=KEEP, scale=-1.0)
+                nc.scalar.activation(dst, src, ACT.Copy, bias=KEEP, scale=-1.0)
+
+        def product(level, h):
+            width = HALF + 2 if level == 1 else HALF
+            double(level, *((0, width - QUARTER), (width - QUARTER, width))[h])
+
+        def double(level, lo, hi):
+            if level == 0:
+                odd = first_share[:, LEAD - 1 + 2 * lo : LEAD - 1 + 2 * hi : 2]
+                for e in range(2):
+                    neighbour = even[:, LEAD - 1 + e + lo : LEAD - 1 + e + hi]
+                    nc.vector.scalar_tensor_tensor(left2[:, e, LEAD + lo : LEAD + hi], odd, -KEEP, neighbour, ALU.add, ALU.mult)
+            elif level == 3:
+                nc.vector.tensor_tensor(
+                    result[0][:, 2 * lo : 2 * hi].rearrange("p (m e) -> p m e", e=2),
+                    first_share[:, LEAD + 2 * lo : LEAD + 2 * hi].rearrange("p (m e) -> p m e", e=2),
+                    left8[:, :, lo:hi].rearrange("p e m -> p m e"),
+                    ALU.mult,
+                )
+            else:
+                src = left2[:, :, 1:] if level == 1 else left4[:]
+                dst = left4[:] if level == 1 else left8[:]
+                nc.vector.tensor_tensor(dst[:, :, lo:hi], src[:, :, lo:hi], src[:, :, lo + level : hi + level], ALU.mult)
+
+        def suffix(b, r):
+            return chains[:, b - 1, r, LEAD:ROW]
+
+        def prefix(b, r):
+            return chains[:, b - 1, GROUP * r, LEAD - 1 : ROW - 1]
 
         def shares(b):
-            for h in range(2):
-                sigmoid(b, h)
-                factor(b, h, False)
+            planes = scores[b][:].rearrange("p (m r) -> p r m", r=GROUP)
+            last = GROUP - 1
+            nc.scalar.activation(share[b][:, last, :], planes[:, last, :], ACT.Sigmoid, bias=minus_one[:])
+            nc.scalar.activation(share[b][:, 0:last, :], planes[:, 0:last, :], ACT.Sigmoid, bias=minus_one[:])
+            nc.scalar.activation(suffix(b, last), share[b][:, last, :], ACT.Copy, bias=-KEEP, scale=1.0)
 
-        def product(b, level, h):
-            src = (left[:, b, :], left2[b][:], left4[b][:], left8[b][:])[level]
-            dst = (left2[b][:], left4[b][:], left8[b][:], result[b][:])[level]
-            width = dst.shape[1]
-            lo, hi = ((0, width - HALF), (width - HALF, width))[h]
-            other = share[b][:, lo:hi] if level == 3 else src[:, lo + 2**level : hi + 2**level]
-            nc.vector.tensor_tensor(dst[:, lo:hi], src[:, lo:hi], other, ALU.mult)
+        def chain(b, step):
+            if step < GROUP - 1:
+                r = GROUP - 2 - step
+                dst, src = suffix(b, r), suffix(b, r + 1)
+            else:
+                r = step - (GROUP - 1)
+                dst, src = prefix(b, r + 1), prefix(b, r)
+            nc.vector.scalar_tensor_tensor(dst, share[b][:, r, :], -KEEP, src, ALU.add, ALU.mult)
+
+        def join(b, h):
+            lo, hi = h * GROUPS // 2, (h + 1) * GROUPS // 2
+            before = chains[:, b - 1, 0 : GROUP * (GROUP - 1) + 1 : GROUP, LEAD - 1 + lo : LEAD - 1 + hi]
+            earlier = chains[:, b - 1, 0:GROUP, LEAD - 2 + lo : LEAD - 2 + hi]
+            nc.vector.tensor_tensor(window[b][:, :, lo:hi], before, earlier, ALU.mult)
+
+        def weigh(b, h):
+            lo, hi = h * GROUPS // 2, (h + 1) * GROUPS // 2
+            nc.vector.tensor_tensor(
+                result[b][:, GROUP * lo : GROUP * hi].rearrange("p (c i r) -> p c r i", i=2, r=GROUP),
+                share[b][:, :, lo:hi].rearrange("p r (c i) -> p c r i", i=2),
+                window[b][:, :, lo:hi].rearrange("p r (c i) -> p c r i", i=2),
+                ALU.mult,
+            )
 
         def store(b, lo, hi):
             nc.sync.dma_start(out[b * P : (b + 1) * P, lo:hi], result[b][:, lo:hi])
 
-        def products(b, levels):
-            for level in levels:
-                for h in range(2):
-                    product(b, level, h)
-
-        load_words(0, 0, T // 2)
-        load_queries(0, 0)
-        load_words(0, T // 2, T)
+        load_words(0, 0, T // 8)
         nc.sync.dma_start(offsets[:], offs)
+        load_words(0, T // 8, T)
+        load_queries(0, 0)
         for q in range(4):
             nc.sync.dma_start(scale_table[32 * q : 32 * q + 8, :].bitcast(I32), x_scales[:, 4 * q : 4 * q + 4, :].bitcast(I32))
         load_queries(1, 0)
@@ -151,9 +214,9 @@ def tile_picked_ystick_eight_p_kernel(tc, x_words, x_scales, hT, offs, out):
             round_queries(g, 0, False)
         nc.vector.quantize_mx(out=first_words[:].bitcast(FP8X4), scales=first_scales[:], in_=first_bf[:])
         for h in range(2):
-            multiply(0, 0, h)
+            multiply(first_scores[h], 0, 0, key_words[0, h], h * HALF, (h + 1) * HALF)
         nc.tensor.matmul_mx(
-            out=banks[3][1][:],
+            out=spare[:],
             lhsT=h_words[0, 0].bitcast(FP8X4),
             lhsT_scale=h_scales[0, 0],
             rhs=first_keys[:].bitcast(FP8X4),
@@ -165,8 +228,9 @@ def tile_picked_ystick_eight_p_kernel(tc, x_words, x_scales, hT, offs, out):
         for h in range(2):
             key_words[1, h] = placed([P, HALF], U32, f"second_keys{h}", at_round0 - KIB // 2 + h * KIB)[:]
             gather_words(key_words[1, h], 1, h * HALF, (h + 1) * HALF)
-            multiply(0, 1, h)
-            sigmoid(0, h)
+            multiply(first_scores[h], 0, 1, key_words[1, h], h * HALF, (h + 1) * HALF)
+            nc.scalar.activation(first_share[:, LEAD + h * HALF : LEAD + (h + 1) * HALF], first_scores[h], ACT.Sigmoid, bias=minus_one[:])
+
         def quantize_block(b, offset):
             words = placed([P, PASSES * P], U32, f"h_words{b}", offset)
             planes = pool.tile([P, PASSES * P], U8, name=f"h_scales{b}", align_bytes=64)
@@ -174,9 +238,7 @@ def tile_picked_ystick_eight_p_kernel(tc, x_words, x_scales, hT, offs, out):
             for g in range(PASSES):
                 h_words[g, b] = words[:, g * P : (g + 1) * P]
                 h_scales[g, b] = planes[:, g * P : (g + 1) * P]
-            for h in range(2):
-                for g in range(PASSES):
-                    multiply(b, g, h)
+                multiply_pass(b, g)
 
         def round_block(b, offset, on_vector):
             rounded[b] = placed([P, PASSES * P * PACK], BF16, f"rounded{b}", offset)
@@ -184,56 +246,67 @@ def tile_picked_ystick_eight_p_kernel(tc, x_words, x_scales, hT, offs, out):
                 h_bf[g, b] = rounded[b][:, g * P * PACK : (g + 1) * P * PACK]
                 round_queries(g, b, on_vector[g])
 
-        def whole(b, level):
-            src = (left[:, b, :], left2[b][:], left4[b][:], left8[b][:])[level]
-            dst = (left2[b][:], left4[b][:], left8[b][:], result[b][:])[level]
-            width = dst.shape[1]
-            other = share[b][:] if level == 3 else src[:, 2**level : width + 2**level]
-            nc.vector.tensor_tensor(dst, src[:, 0:width], other, ALU.mult)
-
         def quantize_pass(g, b, offset):
             h_words[g, b] = placed([P, P], U32, f"h_words{g}_{b}", offset)[:]
             h_scales[g, b] = pool.tile([P, P], U8, name=f"h_scales{g}_{b}", align_bytes=64)[:]
             nc.vector.quantize_mx(out=h_words[g, b].bitcast(FP8X4), scales=h_scales[g, b], in_=h_bf[g, b])
-            for h in range(2):
-                multiply(b, g, h)
+            multiply_pass(b, g)
+
+        def round_pass(g, b, offset, on_vector):
+            h_bf[g, b] = placed([P, P * PACK], BF16, f"rounded{g}_{b}", offset)[:]
+            round_queries(g, b, on_vector)
 
         rounded = {}
-        h_bf[0, 1] = placed([P, P * PACK], BF16, "rounded0_1", at_scales0)[:]
-        h_bf[1, 1] = placed([P, P * PACK], BF16, "rounded1_1", at_words1)[:]
-        round_queries(0, 1, False)
+        round_pass(0, 1, at_scales0, False)
         quantize_pass(0, 1, at_words1 + KIB)
-        round_queries(1, 1, True)
-        factor(0, 0, True)
+        round_pass(1, 1, at_words1, True)
+        round_pass(0, 2, at_words1 + 2 * KIB, True)
         quantize_pass(1, 1, at_codes1)
-        product(0, 0, 0)
-        product(0, 1, 0)
-        factor(0, 1, False)
-        round_block(2, at_planes0, (False, False))
+        factor(0, True)
+        quantize_pass(0, 2, at_codes2)
+        round_pass(1, 2, at_planes0, False)
         shares(1)
-        round_block(3, at_codes1, (False, False))
-        product(0, 0, 1)
-        product(0, 2, 0)
-        product(0, 1, 1)
-        product(0, 3, 0)
-        product(0, 2, 1)
-        quantize_block(2, at_codes2)
-        product(0, 3, 1)
-        store(0, 0, S)
+        product(0, 0)
+        factor(1, True)
+        product(1, 0)
+        product(0, 1)
+        quantize_pass(1, 2, at_codes2 + KIB // 2)
+        round_block(3, at_planes0, (False, False))
         shares(2)
-
-        products(1, (0, 1))
+        product(2, 0)
+        chain(1, 0)
+        product(1, 1)
+        chain(1, 1)
+        product(3, 0)
+        chain(1, 2)
         quantize_block(3, at_codes2 + KIB)
         shares(3)
-        products(1, (2, 3))
+        chain(1, 3)
+        product(2, 1)
+        chain(1, 4)
+        chain(2, 0)
+        chain(1, 5)
+        double(3, QUARTER, QUARTER + QUARTER // 2)
+        chain(2, 1)
+        double(3, QUARTER + QUARTER // 2, HALF)
+        store(0, 0, S)
+        for h in range(2):
+            chain(2, 2 + h)
+            join(1, h)
+        for h in range(2):
+            chain(2, 4 + h)
+            chain(3, h)
+            weigh(1, h)
         store(1, 0, S)
-
-        products(2, (0, 1))
-        whole(3, 0)
-        whole(2, 2)
-        whole(3, 1)
-        whole(2, 3)
+        for h in range(2):
+            chain(3, 2 + h)
+            join(2, h)
+        for h in range(2):
+            chain(3, 4 + h)
+            weigh(2, h)
         store(2, 0, S)
-        products(3, (2, 3))
-        store(3, 0, HALF)
-        store(3, HALF, S)
+        for h in range(2):
+            join(3, h)
+        for h in range(2):
+            weigh(3, h)
+            store(3, h * HALF, (h + 1) * HALF)

@@ -186,10 +186,10 @@ def tile_picked_ystick_eight_p_kernel(tc, x_words, x_scales, hT, offs, out):
         def store(b, lo, hi):
             nc.sync.dma_start(out[b * P : (b + 1) * P, lo:hi], result[b][:, lo:hi])
 
-        load_words(0, 0, T // 8)
-        nc.sync.dma_start(offsets[:], offs)
-        load_words(0, T // 8, T)
+        load_words(0, 0, T // 2)
         load_queries(0, 0)
+        load_words(0, T // 2, T)
+        nc.sync.dma_start(offsets[:], offs)
         for q in range(4):
             nc.sync.dma_start(scale_table[32 * q : 32 * q + 8, :].bitcast(I32), x_scales[:, 4 * q : 4 * q + 4, :].bitcast(I32))
         load_queries(1, 0)

@@ -37,7 +37,7 @@ def tile_picked_ystick_eight_p_kernel(tc, x_words, x_scales, hT, offs, out):
 
         KIB = 1024
         at_words1, at_codes0, at_scales0, at_round0, at_planes0 = 0, 8 * KIB, 9 * KIB, 11 * KIB, 13 * KIB
-        at_codes1, at_codes2, at_raw = 15 * KIB, 17 * KIB, 20 * KIB
+        at_codes1, at_codes2, at_raw, at_left2, at_left4 = 15 * KIB, 17 * KIB, 20 * KIB, 36 * KIB, 39 * KIB
 
         def placed(shape, dtype, name, offset):
             return reused.tile(shape, dtype, name=name, offset=offset, align_bytes=64)
@@ -50,8 +50,8 @@ def tile_picked_ystick_eight_p_kernel(tc, x_words, x_scales, hT, offs, out):
         later = range(1, BLOCKS)
         first_share = pool.tile([P, LEAD + S], F32, name="first_share")
         even = pool.tile([P, LEAD + HALF], F32, name="even")
-        left2 = pool.tile([P, 2, LEAD + HALF], F32, name="left2")
-        left4 = pool.tile([P, 2, LEAD + HALF], F32, name="left4")
+        left2 = placed([P, 2, LEAD + HALF], F32, "left2", at_left2)
+        left4 = placed([P, 2, LEAD + HALF], F32, "left4", at_left4)
         left8 = pool.tile([P, 2, HALF], F32, name="left8")
         share = {1: placed([P, GROUP, GROUPS], F32, "share1", at_raw + 2 * KIB * (PASSES * 2 + 1))}
         share.update({b: pool.tile([P, GROUP, GROUPS], F32, name=f"share{b}") for b in range(2, BLOCKS)})
@@ -186,10 +186,10 @@ def tile_picked_ystick_eight_p_kernel(tc, x_words, x_scales, hT, offs, out):
         def store(b, lo, hi):
             nc.sync.dma_start(out[b * P : (b + 1) * P, lo:hi], result[b][:, lo:hi])
 
-        load_words(0, 0, T // 2)
-        load_queries(0, 0)
-        load_words(0, T // 2, T)
+        load_words(0, 0, T // 8)
         nc.sync.dma_start(offsets[:], offs)
+        load_words(0, T // 8, T)
+        load_queries(0, 0)
         for q in range(4):
             nc.sync.dma_start(scale_table[32 * q : 32 * q + 8, :].bitcast(I32), x_scales[:, 4 * q : 4 * q + 4, :].bitcast(I32))
         load_queries(1, 0)
@@ -231,21 +231,6 @@ def tile_picked_ystick_eight_p_kernel(tc, x_words, x_scales, hT, offs, out):
             multiply(first_scores[h], 0, 1, key_words[1, h], h * HALF, (h + 1) * HALF)
             nc.scalar.activation(first_share[:, LEAD + h * HALF : LEAD + (h + 1) * HALF], first_scores[h], ACT.Sigmoid, bias=minus_one[:])
 
-        def quantize_block(b, offset):
-            words = placed([P, PASSES * P], U32, f"h_words{b}", offset)
-            planes = pool.tile([P, PASSES * P], U8, name=f"h_scales{b}", align_bytes=64)
-            nc.vector.quantize_mx(out=words[:].bitcast(FP8X4), scales=planes[:], in_=rounded[b][:])
-            for g in range(PASSES):
-                h_words[g, b] = words[:, g * P : (g + 1) * P]
-                h_scales[g, b] = planes[:, g * P : (g + 1) * P]
-                multiply_pass(b, g)
-
-        def round_block(b, offset, on_vector):
-            rounded[b] = placed([P, PASSES * P * PACK], BF16, f"rounded{b}", offset)
-            for g in range(PASSES):
-                h_bf[g, b] = rounded[b][:, g * P * PACK : (g + 1) * P * PACK]
-                round_queries(g, b, on_vector[g])
-
         def quantize_pass(g, b, offset):
             h_words[g, b] = placed([P, P], U32, f"h_words{g}_{b}", offset)[:]
             h_scales[g, b] = pool.tile([P, P], U8, name=f"h_scales{g}_{b}", align_bytes=64)[:]
@@ -256,46 +241,47 @@ def tile_picked_ystick_eight_p_kernel(tc, x_words, x_scales, hT, offs, out):
             h_bf[g, b] = placed([P, P * PACK], BF16, f"rounded{g}_{b}", offset)[:]
             round_queries(g, b, on_vector)
 
-        rounded = {}
         round_pass(0, 1, at_scales0, False)
-        quantize_pass(0, 1, at_words1 + KIB)
         round_pass(1, 1, at_words1, True)
-        round_pass(0, 2, at_words1 + 2 * KIB, True)
+        quantize_pass(0, 1, at_words1 + KIB)
         quantize_pass(1, 1, at_codes1)
         factor(0, True)
-        quantize_pass(0, 2, at_codes2)
+        round_pass(0, 2, at_codes0, True)
         round_pass(1, 2, at_planes0, False)
         shares(1)
         product(0, 0)
+        quantize_pass(0, 2, at_codes2)
         factor(1, True)
         product(1, 0)
         product(0, 1)
-        quantize_pass(1, 2, at_codes2 + KIB // 2)
-        round_block(3, at_planes0, (False, False))
+        quantize_pass(1, 2, at_codes2 + KIB)
+        round_pass(0, 3, at_planes0 - KIB // 2, False)
+        round_pass(1, 3, at_planes0 + KIB // 2, False)
         shares(2)
         product(2, 0)
-        chain(1, 0)
         product(1, 1)
-        chain(1, 1)
         product(3, 0)
-        chain(1, 2)
-        quantize_block(3, at_codes2 + KIB)
-        shares(3)
-        chain(1, 3)
+        chain(1, 0)
         product(2, 1)
+        chain(1, 1)
+        quantize_pass(0, 3, at_left2)
+        chain(1, 2)
+        double(3, QUARTER, QUARTER + QUARTER // 2)
+        chain(1, 3)
+        quantize_pass(1, 3, at_left4)
+        shares(3)
         chain(1, 4)
         chain(2, 0)
-        chain(1, 5)
-        double(3, QUARTER, QUARTER + QUARTER // 2)
-        chain(2, 1)
         double(3, QUARTER + QUARTER // 2, HALF)
         store(0, 0, S)
+        chain(1, 5)
         for h in range(2):
-            chain(2, 2 + h)
+            chain(2, 1 + h)
             join(1, h)
+        chain(2, 3)
         for h in range(2):
-            chain(2, 4 + h)
             chain(3, h)
+            chain(2, 4 + h)
             weigh(1, h)
         store(1, 0, S)
         for h in range(2):

@@ -37,7 +37,7 @@ def tile_picked_ystick_eight_p_kernel(tc, x_words, x_scales, hT, offs, out):
 
         KIB = 1024
         at_words1, at_codes0, at_scales0, at_round0, at_planes0 = 0, 8 * KIB, 9 * KIB, 11 * KIB, 13 * KIB
-        at_codes1, at_codes2, at_raw, at_left2, at_left4 = 15 * KIB, 17 * KIB, 20 * KIB, 36 * KIB, 39 * KIB
+        at_codes1, at_codes2, at_raw, at_left2 = 15 * KIB, 17 * KIB, 20 * KIB, 36 * KIB
 
         def placed(shape, dtype, name, offset):
             return reused.tile(shape, dtype, name=name, offset=offset, align_bytes=64)
@@ -51,7 +51,7 @@ def tile_picked_ystick_eight_p_kernel(tc, x_words, x_scales, hT, offs, out):
         first_share = pool.tile([P, LEAD + S], F32, name="first_share")
         even = pool.tile([P, LEAD + HALF], F32, name="even")
         left2 = placed([P, 2, LEAD + HALF], F32, "left2", at_left2)
-        left4 = placed([P, 2, LEAD + HALF], F32, "left4", at_left4)
+        left4 = pool.tile([P, 2, LEAD + HALF], F32, name="left4")
         left8 = pool.tile([P, 2, HALF], F32, name="left8")
         share = {1: placed([P, GROUP, GROUPS], F32, "share1", at_raw + 2 * KIB * (PASSES * 2 + 1))}
         share.update({b: pool.tile([P, GROUP, GROUPS], F32, name=f"share{b}") for b in range(2, BLOCKS)})
@@ -186,10 +186,10 @@ def tile_picked_ystick_eight_p_kernel(tc, x_words, x_scales, hT, offs, out):
         def store(b, lo, hi):
             nc.sync.dma_start(out[b * P : (b + 1) * P, lo:hi], result[b][:, lo:hi])
 
-        load_words(0, 0, T // 8)
-        nc.sync.dma_start(offsets[:], offs)
-        load_words(0, T // 8, T)
+        load_words(0, 0, T // 2)
         load_queries(0, 0)
+        load_words(0, T // 2, T)
+        nc.sync.dma_start(offsets[:], offs)
         for q in range(4):
             nc.sync.dma_start(scale_table[32 * q : 32 * q + 8, :].bitcast(I32), x_scales[:, 4 * q : 4 * q + 4, :].bitcast(I32))
         load_queries(1, 0)
@@ -255,40 +255,40 @@ def tile_picked_ystick_eight_p_kernel(tc, x_words, x_scales, hT, offs, out):
         product(1, 0)
         product(0, 1)
         quantize_pass(1, 2, at_codes2 + KIB)
-        round_pass(0, 3, at_planes0 - KIB // 2, False)
-        round_pass(1, 3, at_planes0 + KIB // 2, False)
+        round_pass(0, 3, at_planes0, False)
         shares(2)
         product(2, 0)
         product(1, 1)
         product(3, 0)
         chain(1, 0)
-        product(2, 1)
+        round_pass(1, 3, at_left2 + KIB, True)
         chain(1, 1)
         quantize_pass(0, 3, at_left2)
-        chain(1, 2)
-        double(3, QUARTER, QUARTER + QUARTER // 2)
-        chain(1, 3)
-        quantize_pass(1, 3, at_left4)
+        quantize_pass(1, 3, at_left2 + KIB // 2)
         shares(3)
-        chain(1, 4)
+        chain(1, 2)
+        product(2, 1)
+        chain(1, 3)
         chain(2, 0)
-        double(3, QUARTER + QUARTER // 2, HALF)
+        product(3, 1)
         store(0, 0, S)
-        chain(1, 5)
+        for step in range(2):
+            chain(1, 4 + step)
+            chain(2, 1 + step)
         for h in range(2):
-            chain(2, 1 + h)
             join(1, h)
-        chain(2, 3)
-        for h in range(2):
+            chain(2, 3 + h)
             chain(3, h)
-            chain(2, 4 + h)
-            weigh(1, h)
+        weigh(1, 0)
+        chain(2, 5)
+        chain(3, 2)
+        weigh(1, 1)
         store(1, 0, S)
         for h in range(2):
-            chain(3, 2 + h)
+            chain(3, 3 + h)
             join(2, h)
+        chain(3, 5)
         for h in range(2):
-            chain(3, 4 + h)
             weigh(2, h)
         store(2, 0, S)
         for h in range(2):

@@ -278,19 +278,19 @@ def tile_picked_ystick_eight_p_kernel(tc, x_words, x_scales, hT, offs, out):
         for h in range(2):
             join(1, h)
             chain(2, 3 + h)
-            chain(3, h)
+        chain(3, 0)
         weigh(1, 0)
         chain(2, 5)
-        chain(3, 2)
+        chain(3, 1)
         weigh(1, 1)
         store(1, 0, S)
         for h in range(2):
-            chain(3, 3 + h)
+            chain(3, 2 + h)
             join(2, h)
-        chain(3, 5)
         for h in range(2):
+            chain(3, 4 + h)
             weigh(2, h)
-        store(2, 0, S)
+            store(2, h * HALF, (h + 1) * HALF)
         for h in range(2):
             join(3, h)
         for h in range(2):

@@ -39,17 +39,19 @@ def tile_picked_ystick_eight_p_kernel(tc, x_words, x_scales, hT, offs, out):
         at_words1, at_codes0, at_scales0, at_round0, at_planes0 = 0, 8 * KIB, 9 * KIB, 11 * KIB, 13 * KIB
         at_codes1, at_codes2, at_raw, at_left2 = 15 * KIB, 17 * KIB, 20 * KIB, 36 * KIB
 
+        at_words0 = 40 * KIB
+
         def placed(shape, dtype, name, offset):
             return reused.tile(shape, dtype, name=name, offset=offset, align_bytes=64)
 
         offsets = pool.tile([P, S // 16], U16, name="offsets")
         scale_table = placed([P, T], U8, "scale_table", at_scales0)
-        word_table = [pool.tile([P, T], U32, name="word_table0", align_bytes=64), placed([P, T], U32, "word_table1", at_words1)]
+        word_table = [placed([P, T], U32, "word_table0", at_words0), placed([P, T], U32, "word_table1", at_words1)]
         key_scales = pool.tile([P, S], U8, name="key_scales", align_bytes=64)
         h_raw = {(g, b): placed([P, PACK, P], F32, f"h_raw{g}_{b}", at_raw + 2 * KIB * (PASSES * b + g)) for b in range(BLOCKS) for g in range(PASSES)}
         later = range(1, BLOCKS)
         first_share = pool.tile([P, LEAD + S], F32, name="first_share")
-        even = pool.tile([P, LEAD + HALF], F32, name="even")
+        one = pool.tile([P, 1], F32, name="one")
         left2 = placed([P, 2, LEAD + HALF], F32, "left2", at_left2)
         left4 = pool.tile([P, 2, LEAD + HALF], F32, name="left4")
         left8 = pool.tile([P, 2, HALF], F32, name="left8")
@@ -59,20 +61,21 @@ def tile_picked_ystick_eight_p_kernel(tc, x_words, x_scales, hT, offs, out):
         window = {b: pool.tile([P, GROUP, GROUPS], F32, name=f"window{b}") for b in later}
         result = [pool.tile([P, S], F32, name=f"result{b}") for b in range(BLOCKS)]
         minus_one = pool.tile([P, 1], F32, name="minus_one")
+        first_bias = placed([P, 1], F32, "first_bias", at_planes0)
         large = pool.tile([P, 1], F32, name="large")
         first_scores = [psum.tile([P, S], F32, name=f"first_scores{h}")[:, 0:HALF] for h in range(2)]
         scores = {b: psum.tile([P, S], F32, name=f"scores{b}") for b in later}
-        spare = psum.tile([P, S], F32, name="spare")
         key_words, h_bf, h_words, h_scales = {}, {}, {}, {}
 
-        nc.vector.memset(scale_table[:].bitcast(I32), 0)
+        nc.gpsimd.memset(scale_table[:].bitcast(I32), 0)
         nc.gpsimd.memset(large[:], 64.0)
         nc.gpsimd.memset(minus_one[:], -1.0)
-        nc.vector.memset(left2[:, :, 1:LEAD], -1.0)
+        nc.gpsimd.memset(first_bias[:], -1.0)
+        nc.vector.memset(left2[:, :, 1 : LEAD + 1], -1.0)
         nc.vector.memset(chains[:, :, 0:GROUP:2, LEAD - 2 : LEAD], 1.0)
         nc.vector.memset(chains[:, :, 1:GROUP:2, LEAD - 2 : LEAD], -1.0)
-        nc.scalar.activation(even[:, LEAD - 1 : LEAD], large[:], ACT.Sigmoid)
-        nc.scalar.activation(first_share[:, LEAD - 1 : LEAD], even[:, LEAD - 1 : LEAD], ACT.Copy, scale=KEEP - 1.0)
+        nc.scalar.activation(one[:], large[:], ACT.Sigmoid)
+        nc.scalar.activation(first_share[:, LEAD - 1 : LEAD], one[:], ACT.Copy, scale=KEEP - 1.0)
 
         def load_words(g, lo, hi):
             words = x_words[g].rearrange("p n t -> p (n t)").bitcast(I32)
@@ -93,15 +96,15 @@ def tile_picked_ystick_eight_p_kernel(tc, x_words, x_scales, hT, offs, out):
             else:
                 nc.scalar.copy(dst, src)
 
-        def multiply(target, b, g, keys, lo, hi):
+        def multiply(target, b, g, keys, lo, hi, opens):
             nc.tensor.matmul_mx(
                 out=target,
                 lhsT=h_words[g, b].bitcast(FP8X4),
                 lhsT_scale=h_scales[g, b],
                 rhs=keys.bitcast(FP8X4),
                 rhs_scale=key_scales[4 * g : P, lo:hi],
-                start=(g == 0),
-                stop=(g == PASSES - 1),
+                start=opens,
+                stop=not opens,
             )
 
         def multiply_pass(b, g):
@@ -130,10 +133,11 @@ def tile_picked_ystick_eight_p_kernel(tc, x_words, x_scales, hT, offs, out):
 
         def double(level, lo, hi):
             if level == 0:
-                odd = first_share[:, LEAD - 1 + 2 * lo : LEAD - 1 + 2 * hi : 2]
                 for e in range(2):
-                    neighbour = even[:, LEAD - 1 + e + lo : LEAD - 1 + e + hi]
-                    nc.vector.scalar_tensor_tensor(left2[:, e, LEAD + lo : LEAD + hi], odd, -KEEP, neighbour, ALU.add, ALU.mult)
+                    first = max(lo, 1 - e)
+                    odd = first_share[:, LEAD - 1 + 2 * first : LEAD - 1 + 2 * hi : 2]
+                    neighbour = even[:, LEAD - 1 + e + first : LEAD - 1 + e + hi]
+                    nc.vector.scalar_tensor_tensor(left2[:, e, LEAD + first : LEAD + hi], odd, -KEEP, neighbour, ALU.add, ALU.mult)
             elif level == 3:
                 nc.vector.tensor_tensor(
                     result[0][:, 2 * lo : 2 * hi].rearrange("p (m e) -> p m e", e=2),
@@ -168,6 +172,10 @@ def tile_picked_ystick_eight_p_kernel(tc, x_words, x_scales, hT, offs, out):
                 dst, src = prefix(b, r + 1), prefix(b, r)
             nc.vector.scalar_tensor_tensor(dst, share[b][:, r, :], -KEEP, src, ALU.add, ALU.mult)
 
+        def chain_block(b):
+            for step in range(2 * (GROUP - 1)):
+                chain(b, step)
+
         def join(b, h):
             lo, hi = h * GROUPS // 2, (h + 1) * GROUPS // 2
             before = chains[:, b - 1, 0 : GROUP * (GROUP - 1) + 1 : GROUP, LEAD - 1 + lo : LEAD - 1 + hi]
@@ -187,66 +195,51 @@ def tile_picked_ystick_eight_p_kernel(tc, x_words, x_scales, hT, offs, out):
             nc.sync.dma_start(out[b * P : (b + 1) * P, lo:hi], result[b][:, lo:hi])
 
         load_words(0, 0, T // 2)
-        load_queries(0, 0)
-        load_words(0, T // 2, T)
         nc.sync.dma_start(offsets[:], offs)
         for q in range(4):
             nc.sync.dma_start(scale_table[32 * q : 32 * q + 8, :].bitcast(I32), x_scales[:, 4 * q : 4 * q + 4, :].bitcast(I32))
-        load_queries(1, 0)
+        load_words(0, T // 2, T)
         load_words(1, 0, T)
+        for g in reversed(range(PASSES)):
+            load_queries(g, 0)
         for b in range(1, BLOCKS):
             for g in range(PASSES):
                 load_queries(g, b)
 
-        first_keys = pool.tile([P, S], U32, name="first_keys", align_bytes=64)
-        gather_words(first_keys[:], 0, 0, S)
-        for h in range(2):
-            key_words[0, h] = first_keys[:, h * HALF : (h + 1) * HALF]
+        keys = [placed([P, S], U32, "first_keys", at_scales0), pool.tile([P, S], U32, name="second_keys", align_bytes=64)]
         nc.vector.tensor_copy(key_scales[:], scale_table[:].indirect(offsets[:]))
-
-        first_bf = placed([P, PASSES * P * PACK], BF16, "first_bf", at_round0)
-        first_words = placed([P, PASSES * P], U32, "first_words", at_codes0)
-        first_scales = placed([P, PASSES * P], U8, "first_scales", at_planes0)
+        gather_words(keys[0][:], 0, 0, S)
+        gather_words(keys[1][:], 1, 0, S)
         for g in range(PASSES):
-            h_bf[g, 0] = first_bf[:, g * P * PACK : (g + 1) * P * PACK]
-            h_words[g, 0] = first_words[:, g * P : (g + 1) * P]
-            h_scales[g, 0] = first_scales[:, g * P : (g + 1) * P]
-            round_queries(g, 0, False)
-        nc.vector.quantize_mx(out=first_words[:].bitcast(FP8X4), scales=first_scales[:], in_=first_bf[:])
-        for h in range(2):
-            multiply(first_scores[h], 0, 0, key_words[0, h], h * HALF, (h + 1) * HALF)
-        nc.tensor.matmul_mx(
-            out=spare[:],
-            lhsT=h_words[0, 0].bitcast(FP8X4),
-            lhsT_scale=h_scales[0, 0],
-            rhs=first_keys[:].bitcast(FP8X4),
-            rhs_scale=key_scales[:],
-            start=True,
-            stop=True,
-        )
-
-        for h in range(2):
-            key_words[1, h] = placed([P, HALF], U32, f"second_keys{h}", at_round0 - KIB // 2 + h * KIB)[:]
-            gather_words(key_words[1, h], 1, h * HALF, (h + 1) * HALF)
-            multiply(first_scores[h], 0, 1, key_words[1, h], h * HALF, (h + 1) * HALF)
-            nc.scalar.activation(first_share[:, LEAD + h * HALF : LEAD + (h + 1) * HALF], first_scores[h], ACT.Sigmoid, bias=minus_one[:])
+            for h in range(2):
+                key_words[g, h] = keys[g][:, h * HALF : (h + 1) * HALF]
 
         def quantize_pass(g, b, offset):
             h_words[g, b] = placed([P, P], U32, f"h_words{g}_{b}", offset)[:]
             h_scales[g, b] = pool.tile([P, P], U8, name=f"h_scales{g}_{b}", align_bytes=64)[:]
             nc.vector.quantize_mx(out=h_words[g, b].bitcast(FP8X4), scales=h_scales[g, b], in_=h_bf[g, b])
-            multiply_pass(b, g)
+            if b > 0:
+                multiply_pass(b, g)
 
         def round_pass(g, b, offset, on_vector):
             h_bf[g, b] = placed([P, P * PACK], BF16, f"rounded{g}_{b}", offset)[:]
             round_queries(g, b, on_vector)
 
-        round_pass(0, 1, at_scales0, False)
-        round_pass(1, 1, at_words1, True)
+        round_pass(1, 0, at_round0, False)
+        round_pass(0, 0, at_words0, True)
+        quantize_pass(1, 0, at_codes0)
+        quantize_pass(0, 0, at_codes0 + KIB // 2)
+        for h in range(2):
+            for g in (1 - h, h):
+                multiply(first_scores[h], 0, g, key_words[g, h], h * HALF, (h + 1) * HALF, g != h)
+            nc.scalar.activation(first_share[:, LEAD + h * HALF : LEAD + (h + 1) * HALF], first_scores[h], ACT.Sigmoid, bias=(first_bias, minus_one)[h][:])
+        round_pass(0, 1, at_round0, True)
+        round_pass(1, 1, at_words0, True)
         quantize_pass(0, 1, at_words1 + KIB)
         quantize_pass(1, 1, at_codes1)
+        round_pass(0, 2, at_round0, True)
+        even = placed([P, LEAD + HALF], F32, "even", at_words0)
         factor(0, True)
-        round_pass(0, 2, at_codes0, True)
         round_pass(1, 2, at_planes0, False)
         shares(1)
         product(0, 0)
@@ -255,44 +248,34 @@ def tile_picked_ystick_eight_p_kernel(tc, x_words, x_scales, hT, offs, out):
         product(1, 0)
         product(0, 1)
         quantize_pass(1, 2, at_codes2 + KIB)
-        round_pass(0, 3, at_planes0, False)
+        third_bf = placed([P, PASSES * P * PACK], BF16, "third_bf", at_planes0)
+        for g in range(PASSES):
+            h_bf[g, 3] = third_bf[:, g * P * PACK : (g + 1) * P * PACK]
+            round_queries(g, 3, False)
         shares(2)
+        chain_block(1)
         product(2, 0)
         product(1, 1)
-        product(3, 0)
-        chain(1, 0)
-        round_pass(1, 3, at_left2 + KIB, True)
-        chain(1, 1)
-        quantize_pass(0, 3, at_left2)
-        quantize_pass(1, 3, at_left2 + KIB // 2)
+        third_words = placed([P, PASSES * P], U32, "third_words", at_left2)
+        third_scales = pool.tile([P, PASSES * P], U8, name="third_scales", align_bytes=64)
+        nc.vector.quantize_mx(out=third_words[:].bitcast(FP8X4), scales=third_scales[:], in_=third_bf[:])
+        for g in range(PASSES):
+            h_words[g, 3] = third_words[:, g * P : (g + 1) * P]
+            h_scales[g, 3] = third_scales[:, g * P : (g + 1) * P]
+            multiply_pass(3, g)
         shares(3)
-        chain(1, 2)
+        product(3, 0)
         product(2, 1)
-        chain(1, 3)
-        chain(2, 0)
+        for b in range(2, BLOCKS):
+            chain_block(b)
         product(3, 1)
         store(0, 0, S)
-        for step in range(2):
-            chain(1, 4 + step)
-            chain(2, 1 + step)
-        for h in range(2):
-            join(1, h)
-            chain(2, 3 + h)
-        chain(3, 0)
-        weigh(1, 0)
-        chain(2, 5)
-        chain(3, 1)
-        weigh(1, 1)
-        store(1, 0, S)
-        for h in range(2):
-            chain(3, 2 + h)
-            join(2, h)
-        for h in range(2):
-            chain(3, 4 + h)
-            weigh(2, h)
-            store(2, h * HALF, (h + 1) * HALF)
-        for h in range(2):
-            join(3, h)
-        for h in range(2):
-            weigh(3, h)
-            store(3, h * HALF, (h + 1) * HALF)
+        for b in later:
+            for h in range(2):
+                join(b, h)
+            for h in range(2):
+                weigh(b, h)
+                if b > 1:
+                    store(b, h * HALF, (h + 1) * HALF)
+            if b == 1:
+                store(b, 0, S)

@@ -63,9 +63,10 @@ def tile_picked_ystick_eight_p_kernel(tc, x_words, x_scales, hT, offs, out):
         minus_one = pool.tile([P, 1], F32, name="minus_one")
         first_bias = placed([P, 1], F32, "first_bias", at_planes0)
         large = pool.tile([P, 1], F32, name="large")
-        first_scores = [psum.tile([P, S], F32, name=f"first_scores{h}")[:, 0:HALF] for h in range(2)]
+        pieces = ((0, QUARTER), (QUARTER, HALF), (HALF, S))
+        first_scores = [psum.tile([P, S], F32, name=f"first_scores{i}")[:, 0 : hi - lo] for i, (lo, hi) in enumerate(pieces)]
         scores = {b: psum.tile([P, S], F32, name=f"scores{b}") for b in later}
-        key_words, h_bf, h_words, h_scales = {}, {}, {}, {}
+        h_bf, h_words, h_scales = {}, {}, {}
 
         nc.gpsimd.memset(scale_table[:].bitcast(I32), 0)
         nc.gpsimd.memset(large[:], 64.0)
@@ -108,16 +109,7 @@ def tile_picked_ystick_eight_p_kernel(tc, x_words, x_scales, hT, offs, out):
             )
 
         def multiply_pass(b, g):
-            for h in range(2):
-                nc.tensor.matmul_mx(
-                    out=scores[b][:, h * HALF : (h + 1) * HALF],
-                    lhsT=h_words[g, b].bitcast(FP8X4),
-                    lhsT_scale=h_scales[g, b],
-                    rhs=key_words[g, h].bitcast(FP8X4),
-                    rhs_scale=key_scales[4 * g : P, h * HALF : (h + 1) * HALF],
-                    start=(g == 0 and h == 0),
-                    stop=(g == PASSES - 1 and h == 1),
-                )
+            multiply(scores[b][:], b, g, keys[g][:], 0, S, g == 0)
 
         def factor(h, on_vector):
             src = first_share[:, LEAD + h * HALF : LEAD + (h + 1) * HALF : 2]
@@ -210,9 +202,6 @@ def tile_picked_ystick_eight_p_kernel(tc, x_words, x_scales, hT, offs, out):
         nc.vector.tensor_copy(key_scales[:], scale_table[:].indirect(offsets[:]))
         gather_words(keys[0][:], 0, 0, S)
         gather_words(keys[1][:], 1, 0, S)
-        for g in range(PASSES):
-            for h in range(2):
-                key_words[g, h] = keys[g][:, h * HALF : (h + 1) * HALF]
 
         def quantize_pass(g, b, offset):
             h_words[g, b] = placed([P, P], U32, f"h_words{g}_{b}", offset)[:]
@@ -229,17 +218,18 @@ def tile_picked_ystick_eight_p_kernel(tc, x_words, x_scales, hT, offs, out):
         round_pass(0, 0, at_words0, True)
         quantize_pass(1, 0, at_codes0)
         quantize_pass(0, 0, at_codes0 + KIB // 2)
-        for h in range(2):
+        for i, (lo, hi) in enumerate(pieces):
+            h = lo // HALF
             for g in (1 - h, h):
-                multiply(first_scores[h], 0, g, key_words[g, h], h * HALF, (h + 1) * HALF, g != h)
-            nc.scalar.activation(first_share[:, LEAD + h * HALF : LEAD + (h + 1) * HALF], first_scores[h], ACT.Sigmoid, bias=(first_bias, minus_one)[h][:])
+                multiply(first_scores[i], 0, g, keys[g][:, lo:hi], lo, hi, g != h)
+            nc.scalar.activation(first_share[:, LEAD + lo : LEAD + hi], first_scores[i], ACT.Sigmoid, bias=(minus_one, first_bias, minus_one)[i][:])
         round_pass(0, 1, at_round0, True)
         round_pass(1, 1, at_words0, True)
         quantize_pass(0, 1, at_words1 + KIB)
         quantize_pass(1, 1, at_codes1)
-        round_pass(0, 2, at_round0, True)
-        even = placed([P, LEAD + HALF], F32, "even", at_words0)
+        even = placed([P, LEAD + HALF], F32, "even", at_raw + 2 * KIB * (PASSES + 1))
         factor(0, True)
+        round_pass(0, 2, at_round0, True)
         round_pass(1, 2, at_planes0, False)
         shares(1)
         product(0, 0)

@@ -108,8 +108,8 @@ def tile_picked_ystick_eight_p_kernel(tc, x_words, x_scales, hT, offs, out):
                 stop=not opens,
             )
 
-        def multiply_pass(b, g):
-            multiply(scores[b][:], b, g, keys[g][:], 0, S, g == 0)
+        def multiply_pass(b, g, opens):
+            multiply(scores[b][:], b, g, keys[g][:], 0, S, opens)
 
         def factor(h, on_vector):
             src = first_share[:, LEAD + h * HALF : LEAD + (h + 1) * HALF : 2]
@@ -207,8 +207,8 @@ def tile_picked_ystick_eight_p_kernel(tc, x_words, x_scales, hT, offs, out):
             h_words[g, b] = placed([P, P], U32, f"h_words{g}_{b}", offset)[:]
             h_scales[g, b] = pool.tile([P, P], U8, name=f"h_scales{g}_{b}", align_bytes=64)[:]
             nc.vector.quantize_mx(out=h_words[g, b].bitcast(FP8X4), scales=h_scales[g, b], in_=h_bf[g, b])
-            if b > 0:
-                multiply_pass(b, g)
+            if b == 1:
+                multiply_pass(b, g, g == 0)
 
         def round_pass(g, b, offset, on_vector):
             h_bf[g, b] = placed([P, P * PACK], BF16, f"rounded{g}_{b}", offset)[:]
@@ -238,6 +238,8 @@ def tile_picked_ystick_eight_p_kernel(tc, x_words, x_scales, hT, offs, out):
         product(1, 0)
         product(0, 1)
         quantize_pass(1, 2, at_codes2 + KIB)
+        for g in reversed(range(PASSES)):
+            multiply_pass(2, g, g == PASSES - 1)
         third_bf = placed([P, PASSES * P * PACK], BF16, "third_bf", at_planes0)
         for g in range(PASSES):
             h_bf[g, 3] = third_bf[:, g * P * PACK : (g + 1) * P * PACK]
@@ -252,7 +254,7 @@ def tile_picked_ystick_eight_p_kernel(tc, x_words, x_scales, hT, offs, out):
         for g in range(PASSES):
             h_words[g, 3] = third_words[:, g * P : (g + 1) * P]
             h_scales[g, 3] = third_scales[:, g * P : (g + 1) * P]
-            multiply_pass(3, g)
+            multiply_pass(3, g, g == 0)
         shares(3)
         product(3, 0)
         product(2, 1)

@@ -243,11 +243,12 @@ def tile_picked_ystick_eight_p_kernel(tc, x_words, x_scales, hT, offs, out):
         third_bf = placed([P, PASSES * P * PACK], BF16, "third_bf", at_planes0)
         for g in range(PASSES):
             h_bf[g, 3] = third_bf[:, g * P * PACK : (g + 1) * P * PACK]
-            round_queries(g, 3, False)
+        round_queries(0, 3, False)
         shares(2)
         chain_block(1)
         product(2, 0)
         product(1, 1)
+        round_queries(1, 3, True)
         third_words = placed([P, PASSES * P], U32, "third_words", at_left2)
         third_scales = pool.tile([P, PASSES * P], U8, name="third_scales", align_bytes=64)
         nc.vector.quantize_mx(out=third_words[:].bitcast(FP8X4), scales=third_scales[:], in_=third_bf[:])

from contextlib import ExitStack

import concourse.mybir as mybir

K, T, S, V = 1024, 2048, 512, 512
FLOPS = 2 * K * S * V

F32 = mybir.dt.float32
BF16 = mybir.dt.bfloat16
I32 = mybir.dt.int32
U32 = mybir.dt.uint32
U16 = mybir.dt.uint16
U8 = mybir.dt.uint8
FP8X4 = mybir.dt.float8_e4m3fn_x4
ACT = mybir.ActivationFunctionType
ALU = mybir.AluOpType

P = 128
PACK = 4
PASSES = K // (P * PACK)
BLOCKS = V // P
HALF = S // 2
QUARTER = S // 4
LEAD = 4
GROUP = 4
GROUPS = S // GROUP
ROW = LEAD + GROUPS
KEEP = 1.001


def tile_picked_ystick_eight_p_kernel(tc, x_words, x_scales, hT, offs, out):
    nc = tc.nc
    with ExitStack() as ctx:
        pool = ctx.enter_context(tc.tile_pool(name="held", bufs=1))
        reused = ctx.enter_context(tc.tile_pool(name="reused", bufs=1))
        psum = ctx.enter_context(tc.psum_pool(name="psum", bufs=1))

        KIB = 1024
        at_words1, at_codes0, at_scales0, at_round0, at_planes0 = 0, 8 * KIB, 9 * KIB, 11 * KIB, 13 * KIB
        at_codes1, at_codes2, at_raw, at_left2 = 15 * KIB, 17 * KIB, 20 * KIB, 36 * KIB

        at_words0 = 40 * KIB

        def placed(shape, dtype, name, offset):
            return reused.tile(shape, dtype, name=name, offset=offset, align_bytes=64)

        offsets = pool.tile([P, S // 16], U16, name="offsets")
        scale_table = placed([P, T], U8, "scale_table", at_scales0)
        word_table = [placed([P, T], U32, "word_table0", at_words0), placed([P, T], U32, "word_table1", at_words1)]
        key_scales = pool.tile([P, S], U8, name="key_scales", align_bytes=64)
        h_raw = {(g, b): placed([P, PACK, P], F32, f"h_raw{g}_{b}", at_raw + 2 * KIB * (PASSES * b + g)) for b in range(BLOCKS) for g in range(PASSES)}
        later = range(1, BLOCKS)
        first_share = pool.tile([P, LEAD + S], F32, name="first_share")
        one = pool.tile([P, 1], F32, name="one")
        left2 = placed([P, 2, LEAD + HALF], F32, "left2", at_left2)
        left4 = pool.tile([P, 2, LEAD + HALF], F32, name="left4")
        left8 = pool.tile([P, 2, HALF], F32, name="left8")
        share = {1: placed([P, GROUP, GROUPS], F32, "share1", at_raw + 2 * KIB * (PASSES * 2 + 1))}
        share.update({b: pool.tile([P, GROUP, GROUPS], F32, name=f"share{b}") for b in range(2, BLOCKS)})
        chains = pool.tile([P, BLOCKS - 1, 3 * GROUP + 1, ROW], F32, name="chains")
        window = {b: pool.tile([P, GROUP, GROUPS], F32, name=f"window{b}") for b in later}
        result = [pool.tile([P, S], F32, name=f"result{b}") for b in range(BLOCKS)]
        minus_one = pool.tile([P, 1], F32, name="minus_one")
        first_bias = placed([P, 1], F32, "first_bias", at_planes0)
        large = pool.tile([P, 1], F32, name="large")
        pieces = ((0, QUARTER), (QUARTER, HALF), (HALF, S))
        first_scores = [psum.tile([P, S], F32, name=f"first_scores{i}")[:, 0 : hi - lo] for i, (lo, hi) in enumerate(pieces)]
        scores = {b: psum.tile([P, S], F32, name=f"scores{b}") for b in later}
        h_bf, h_words, h_scales = {}, {}, {}

        nc.gpsimd.memset(scale_table[:].bitcast(I32), 0)
        nc.gpsimd.memset(large[:], 64.0)
        nc.gpsimd.memset(minus_one[:], -1.0)
        nc.gpsimd.memset(first_bias[:], -1.0)
        nc.vector.memset(left2[:, :, 1 : LEAD + 1], -1.0)
        nc.vector.memset(chains[:, :, 0:GROUP:2, LEAD - 2 : LEAD], 1.0)
        nc.vector.memset(chains[:, :, 1:GROUP:2, LEAD - 2 : LEAD], -1.0)
        nc.scalar.activation(one[:], large[:], ACT.Sigmoid)
        nc.scalar.activation(first_share[:, LEAD - 1 : LEAD], one[:], ACT.Copy, scale=KEEP - 1.0)

        def load_words(g, lo, hi):
            words = x_words[g].rearrange("p n t -> p (n t)").bitcast(I32)
            nc.sync.dma_start(word_table[g][:, lo:hi].bitcast(I32), words[:, lo:hi])

        def load_queries(g, b):
            rows = hT[g * P * PACK : (g + 1) * P * PACK, b * P : (b + 1) * P]
            nc.sync.dma_start(h_raw[g, b][:], rows.rearrange("(p j) v -> p j v", j=PACK))

        def gather_words(target, g, lo, hi):
            nc.vector.tensor_copy(target, word_table[g][:].indirect(offsets[:, lo // 16 : hi // 16]))

        def round_queries(g, b, on_vector):
            dst = h_bf[g, b].rearrange("p (c i j) -> p c j i", i=4, j=PACK)
            src = h_raw[g, b][:].rearrange("p j (c i) -> p c j i", i=4)
            if on_vector:
                nc.vector.tensor_copy(dst, src)
            else:
                nc.scalar.copy(dst, src)

        def multiply(target, b, g, keys, lo, hi, opens):
            nc.tensor.matmul_mx(
                out=target,
                lhsT=h_words[g, b].bitcast(FP8X4),
                lhsT_scale=h_scales[g, b],
                rhs=keys.bitcast(FP8X4),
                rhs_scale=key_scales[4 * g : P, lo:hi],
                start=opens,
                stop=not opens,
            )

        def multiply_pass(b, g, opens):
            multiply(scores[b][:], b, g, keys[g][:], 0, S, opens)

        def factor(h, on_vector):
            src = first_share[:, LEAD + h * HALF : LEAD + (h + 1) * HALF : 2]
            dst = even[:, LEAD + h * QUARTER : LEAD + (h + 1) * QUARTER]
            if on_vector:
                nc.vector.tensor_scalar(dst, src, -1.0, KEEP, ALU.mult, ALU.add)
            else:
                nc.scalar.activation(dst, src, ACT.Copy, bias=KEEP, scale=-1.0)

        def product(level, h):
            width = HALF + 2 if level == 1 else HALF
            double(level, *((0, width - QUARTER), (width - QUARTER, width))[h])

        def double(level, lo, hi):
            if level == 0:
                for e in range(2):
                    first = max(lo, 1 - e)
                    odd = first_share[:, LEAD - 1 + 2 * first : LEAD - 1 + 2 * hi : 2]
                    neighbour = even[:, LEAD - 1 + e + first : LEAD - 1 + e + hi]
                    nc.vector.scalar_tensor_tensor(left2[:, e, LEAD + first : LEAD + hi], odd, -KEEP, neighbour, ALU.add, ALU.mult)
            elif level == 3:
                nc.vector.tensor_tensor(
                    result[0][:, 2 * lo : 2 * hi].rearrange("p (m e) -> p m e", e=2),
                    first_share[:, LEAD + 2 * lo : LEAD + 2 * hi].rearrange("p (m e) -> p m e", e=2),
                    left8[:, :, lo:hi].rearrange("p e m -> p m e"),
                    ALU.mult,
                )
            else:
                src = left2[:, :, 1:] if level == 1 else left4[:]
                dst = left4[:] if level == 1 else left8[:]
                nc.vector.tensor_tensor(dst[:, :, lo:hi], src[:, :, lo:hi], src[:, :, lo + level : hi + level], ALU.mult)

        def suffix(b, r):
            return chains[:, b - 1, r, LEAD:ROW]

        def prefix(b, r):
            return chains[:, b - 1, GROUP * r, LEAD - 1 : ROW - 1]

        def shares(b):
            planes = scores[b][:].rearrange("p (m r) -> p r m", r=GROUP)
            last = GROUP - 1
            nc.scalar.activation(share[b][:, last, :], planes[:, last, :], ACT.Sigmoid, bias=minus_one[:])
            nc.scalar.activation(share[b][:, 0:last, :], planes[:, 0:last, :], ACT.Sigmoid, bias=minus_one[:])
            nc.scalar.activation(suffix(b, last), share[b][:, last, :], ACT.Copy, bias=-KEEP, scale=1.0)

        def chain(b, step):
            if step < GROUP - 1:
                r = GROUP - 2 - step
                dst, src = suffix(b, r), suffix(b, r + 1)
            else:
                r = step - (GROUP - 1)
                dst, src = prefix(b, r + 1), prefix(b, r)
            nc.vector.scalar_tensor_tensor(dst, share[b][:, r, :], -KEEP, src, ALU.add, ALU.mult)

        def chain_block(b):
            for step in range(2 * (GROUP - 1)):
                chain(b, step)

        def join(b, h):
            lo, hi = h * GROUPS // 2, (h + 1) * GROUPS // 2
            before = chains[:, b - 1, 0 : GROUP * (GROUP - 1) + 1 : GROUP, LEAD - 1 + lo : LEAD - 1 + hi]
            earlier = chains[:, b - 1, 0:GROUP, LEAD - 2 + lo : LEAD - 2 + hi]
            nc.vector.tensor_tensor(window[b][:, :, lo:hi], before, earlier, ALU.mult)

        def weigh(b, h):
            lo, hi = h * GROUPS // 2, (h + 1) * GROUPS // 2
            nc.vector.tensor_tensor(
                result[b][:, GROUP * lo : GROUP * hi].rearrange("p (c i r) -> p c r i", i=2, r=GROUP),
                share[b][:, :, lo:hi].rearrange("p r (c i) -> p c r i", i=2),
                window[b][:, :, lo:hi].rearrange("p r (c i) -> p c r i", i=2),
                ALU.mult,
            )

        def store(b, lo, hi):
            nc.sync.dma_start(out[b * P : (b + 1) * P, lo:hi], result[b][:, lo:hi])

        load_words(0, 0, T // 2)
        nc.sync.dma_start(offsets[:], offs)
        for q in range(4):
            nc.sync.dma_start(scale_table[32 * q : 32 * q + 8, :].bitcast(I32), x_scales[:, 4 * q : 4 * q + 4, :].bitcast(I32))
        load_words(0, T // 2, T)
        load_words(1, 0, T)
        for g in reversed(range(PASSES)):
            load_queries(g, 0)
        for b in range(1, BLOCKS):
            for g in range(PASSES):
                load_queries(g, b)

        keys = [placed([P, S], U32, "first_keys", at_scales0), pool.tile([P, S], U32, name="second_keys", align_bytes=64)]
        nc.vector.tensor_copy(key_scales[:], scale_table[:].indirect(offsets[:]))
        gather_words(keys[0][:], 0, 0, S)
        gather_words(keys[1][:], 1, 0, S)

        def quantize_pass(g, b, offset):
            h_words[g, b] = placed([P, P], U32, f"h_words{g}_{b}", offset)[:]
            h_scales[g, b] = pool.tile([P, P], U8, name=f"h_scales{g}_{b}", align_bytes=64)[:]
            nc.vector.quantize_mx(out=h_words[g, b].bitcast(FP8X4), scales=h_scales[g, b], in_=h_bf[g, b])
            if b == 1:
                multiply_pass(b, g, g == 0)

        def round_pass(g, b, offset, on_vector):
            h_bf[g, b] = placed([P, P * PACK], BF16, f"rounded{g}_{b}", offset)[:]
            round_queries(g, b, on_vector)

        round_pass(1, 0, at_round0, False)
        round_pass(0, 0, at_words0, True)
        quantize_pass(1, 0, at_codes0)
        quantize_pass(0, 0, at_codes0 + KIB // 2)
        for i, (lo, hi) in enumerate(pieces):
            h = lo // HALF
            for g in (1 - h, h):
                multiply(first_scores[i], 0, g, keys[g][:, lo:hi], lo, hi, g != h)
            nc.scalar.activation(first_share[:, LEAD + lo : LEAD + hi], first_scores[i], ACT.Sigmoid, bias=(minus_one, first_bias, minus_one)[i][:])
        round_pass(0, 1, at_round0, True)
        round_pass(1, 1, at_words0, True)
        quantize_pass(0, 1, at_words1 + KIB)
        quantize_pass(1, 1, at_codes1)
        even = placed([P, LEAD + HALF], F32, "even", at_raw + 2 * KIB * (PASSES + 1))
        factor(0, True)
        round_pass(0, 2, at_round0, True)
        round_pass(1, 2, at_planes0, False)
        shares(1)
        product(0, 0)
        quantize_pass(0, 2, at_codes2)
        factor(1, True)
        product(1, 0)
        product(0, 1)
        quantize_pass(1, 2, at_codes2 + KIB)
        for g in reversed(range(PASSES)):
            multiply_pass(2, g, g == PASSES - 1)
        third_bf = placed([P, PASSES * P * PACK], BF16, "third_bf", at_planes0)
        for g in range(PASSES):
            h_bf[g, 3] = third_bf[:, g * P * PACK : (g + 1) * P * PACK]
        round_queries(0, 3, False)
        shares(2)
        chain_block(1)
        product(2, 0)
        product(1, 1)
        round_queries(1, 3, True)
        third_words = placed([P, PASSES * P], U32, "third_words", at_left2)
        third_scales = pool.tile([P, PASSES * P], U8, name="third_scales", align_bytes=64)
        nc.vector.quantize_mx(out=third_words[:].bitcast(FP8X4), scales=third_scales[:], in_=third_bf[:])
        for g in range(PASSES):
            h_words[g, 3] = third_words[:, g * P : (g + 1) * P]
            h_scales[g, 3] = third_scales[:, g * P : (g + 1) * P]
            multiply_pass(3, g, g == 0)
        shares(3)
        product(3, 0)
        product(2, 1)
        for b in range(2, BLOCKS):
            chain_block(b)
        product(3, 1)
        store(0, 0, S)
        for b in later:
            for h in range(2):
                join(b, h)
            for h in range(2):
                weigh(b, h)
                if b > 1:
                    store(b, h * HALF, (h + 1) * HALF)
            if b == 1:
                store(b, 0, S)
